import numpy as np
import ml_dtypes


def mxq(x, axis, fmt="e4m3"):
    dtype, down = {"e4m3": (ml_dtypes.float8_e4m3fn, 7), "e5m2": (ml_dtypes.float8_e5m2, 14)}[fmt]
    v = np.moveaxis(np.asarray(x, np.float32).astype(ml_dtypes.bfloat16).astype(np.float64), axis, -1)
    blocks = v.reshape(v.shape[:-1] + (-1, 32))
    amax = np.abs(blocks).max(-1, keepdims=True)
    byte = np.maximum(np.where(amax > 0, np.frexp(amax)[1] - 1 + 127, 0) - down, 1)
    scale = np.exp2(byte - 127.0)
    codes = (blocks / scale).astype(np.float32).astype(dtype).astype(np.float64)
    return np.moveaxis((codes * scale).reshape(v.shape), -1, axis)


WIDE = False


def mx_kscale(k):
    if not WIDE:
        return np.ones(k)
    levels = np.array([10, -10, 5, -5, 0])
    if k % 512:
        return np.exp2(np.random.permutation(np.resize(levels, k // 32))).repeat(32)
    a = np.empty((k // 512, 16))
    for p in range(k // 512):
        a[p, :8] = np.random.permutation(np.resize(levels, 8))
        for g in range(8):
            far = levels[np.abs(levels - a[p, g]) >= 10]
            a[p, g + 8] = far[np.random.randint(len(far))]
    return np.exp2(a.ravel()).repeat(32)


BF16 = ml_dtypes.bfloat16


def bf(x):
    return np.asarray(x, np.float32).astype(BF16)


def f64(x):
    return np.asarray(x).astype(np.float64)


E2M1 = np.array([0.0, 0.5, 1.0, 1.5, 2.0, 3.0, 4.0, 6.0, -0.0, -0.5, -1.0, -1.5, -2.0, -3.0, -4.0, -6.0])


def pack_weight(w, fmt):
    k, n = w.shape
    w = f64(bf(w)).reshape(k // 32, 32, n)
    amax = np.abs(w).max(1)
    if fmt == "e4m3":
        byte = np.frexp(amax)[1] - 1 + 127 - 7
    else:
        mant, ex = np.frexp(amax / 6.0)
        byte = np.where(mant > 0.5, ex, ex - 1) + 127
    byte = np.clip(np.where(amax > 0, byte, 1), 1, 254)
    scaled = (w * np.exp2(127.0 - byte)[:, None, :]).reshape(k, n).astype(np.float32)
    by_word = np.ascontiguousarray(scaled.reshape(k // 512, 128, 4, n).transpose(0, 1, 3, 2))
    if fmt == "e4m3":
        words = by_word.astype(ml_dtypes.float8_e4m3fn).view(np.uint8)
    else:
        c = by_word.astype(ml_dtypes.float4_e2m1fn).view(np.uint8) & 0xF
        words = c[..., 0::2] | (c[..., 1::2] << 4)
    return np.ascontiguousarray(words), np.ascontiguousarray(byte.astype(np.uint8).reshape(k // 512, 16, n))


def unpack_weight(words, scales, fmt):
    g, p, n, _ = words.shape
    if fmt == "e4m3":
        vals = np.ascontiguousarray(words).view(ml_dtypes.float8_e4m3fn).astype(np.float64)
    else:
        nib = np.empty((g, p, n, 4), np.uint8)
        nib[..., 0::2] = words & 0xF
        nib[..., 1::2] = words >> 4
        vals = E2M1[nib]
    vals = vals * np.repeat(np.exp2(scales.astype(np.float64) - 127.0), 8, axis=1)[..., None]
    return vals.transpose(0, 1, 3, 2).reshape(g * 512, n)
def pack4(w):
    words, scales = pack_weight(w, "e2m1")
    return words.reshape(words.shape[0], 128, -1), scales


def unpack4(words, scales):
    return unpack_weight(words.reshape(words.shape[0], 128, -1, 2), scales, "e2m1")


def planes(Y):
    n, m = Y.shape
    b = f64(bf(Y)).reshape(n // 32, 32, m)
    amax = np.abs(b).max(1)
    byte = np.clip(np.where(amax > 0, np.frexp(amax)[1] - 1 + 127 - 7, 1), 1, 254)
    codes = (b * np.exp2(127.0 - byte)[:, None, :]).reshape(n, m).astype(np.float32).astype(ml_dtypes.float8_e4m3fn).view(np.uint8)
    words = codes.reshape(n // 512, 128, 4, m).transpose(0, 1, 3, 2)
    return np.ascontiguousarray(words), np.ascontiguousarray(byte.astype(np.uint8).reshape(n // 512, 16, m))


B, D, H, N, T = 1024, 1024, 512, 1024, 3


def sigmoid(v):
    return 1.0 / (1.0 + np.exp(-v))


def setup_inputs():
    s, t = mx_kscale(D), mx_kscale(H)
    x = bf(np.random.standard_normal((B, D)) * s)
    w_words, w_scales = pack4(np.random.standard_normal((D, H)) / np.sqrt(D) / s[:, None])
    return {"x": x,
            "w_words": w_words,
            "w_scales": w_scales,
            "g": bf((1.0 + 0.1 * np.random.standard_normal(H)) * t),
            "wh": bf(np.random.standard_normal((T, H, N)) * 1.5 / np.sqrt(H) / t[None, :, None]),
            "o": bf(np.random.uniform(0.0, 1.0, (B, N))),
            "y": bf(np.random.uniform(0.0, 1.0, (B, N)))}


def shared_trunk(x, w_words, w_scales, g):
    return f64(g)[None, :] * np.tanh(mxq(f64(x), 1, "e4m3") @ unpack4(w_words, w_scales))


def core(x, w_words, w_scales, g, wh, o, y):
    h = shared_trunk(x, w_words, w_scales, g)
    z = mxq(h, 1, "e4m3") @ mxq(f64(wh), 1, "e4m3")
    p = np.maximum(sigmoid(z[0]), 0.2)
    err = np.square(f64(y) - sigmoid(z[1]))
    e = z[2]
    return e + f64(o) * (err - e) / p


def reference(x, w_words, w_scales, g, wh, o, y):
    R_out = core(x, w_words, w_scales, g, wh, o, y)
    words, scales = planes(R_out.T)
    return R_out, words, scales

@@ -1,0 +1,429 @@
+from contextlib import ExitStack
+
+import concourse.mybir as mybir
+from concourse.masks import make_identity
+
+F32 = mybir.dt.float32
+BF16 = mybir.dt.bfloat16
+U32 = mybir.dt.uint32
+I32 = mybir.dt.int32
+U8 = mybir.dt.uint8
+FP8X4 = mybir.dt.float8_e4m3fn_x4
+FP4X4 = mybir.dt.float4_e2m1fn_x4
+ACT = mybir.ActivationFunctionType
+ALU = mybir.AluOpType
+
+P = 128
+B, D, H, N, T = 1024, 1024, 512, 1024, 3
+ROWS = B // P
+HALF = 512
+FLOPS = 2 * B * D * H + T * 2 * B * H * N
+
+
+def tile_escmdoublyrobusterrormap_x2_kernel(tc, x, w_words, w_scales, g, wh, o, y, out_0, out_1, out_2):
+    nc = tc.nc
+    with ExitStack() as ctx:
+        const = ctx.enter_context(tc.tile_pool(name="const", bufs=1))
+        ld = ctx.enter_context(tc.tile_pool(name="ld", bufs=8))
+        wraw = ctx.enter_context(tc.tile_pool(name="wraw", bufs=6))
+        st = ctx.enter_context(tc.tile_pool(name="st", bufs=2))
+        st3 = ctx.enter_context(tc.tile_pool(name="st3", bufs=3))
+        ps_1 = ctx.enter_context(tc.psum_pool(name="ps1", bufs=1))
+        ps_2 = ctx.enter_context(tc.psum_pool(name="ps2", bufs=2))
+
+        ident = const.tile([P, P], F32, name="ident", align_bytes=64)
+        minus2 = const.tile([P, P], BF16, name="minus2", align_bytes=64)
+        warm = const.tile([P, 1], F32, name="warm")
+        w_codes = const.tile([P, 2, 2 * H], U8, name="w_codes", align_bytes=64)
+        w_plane = const.tile([P, 2, H], U8, name="w_plane", align_bytes=64)
+        gain = const.tile([P, 4], BF16, name="gain", align_bytes=64)
+
+        nc.vector.memset(w_plane[:].rearrange("p g n -> p (g n)").bitcast(I32), 0)
+        nc.vector.memset(warm[:], 0.0)
+        make_identity(nc, ident[:])
+        nc.scalar.activation(out=warm[:], in_=warm[:], func=ACT.Exp)
+        nc.vector.tensor_scalar(out=minus2[:], in0=ident[:], scalar1=-2.0, scalar2=None, op0=ALU.mult)
+
+        x_sb, o_sb, y_sb, wh_raw = {}, {}, {}, {}
+
+        def load_x(r):
+            x_sb[r] = ld.tile([P, D], BF16, name="x_sb", align_bytes=64)
+            nc.sync.dma_start(out=x_sb[r][:], in_=x[P * r : P * (r + 1), :])
+
+        def load_oy(r):
+            o_sb[r] = ld.tile([P, N], BF16, name="o_sb", align_bytes=64)
+            nc.sync.dma_start(out=o_sb[r][:], in_=o[P * r : P * (r + 1), :])
+            y_sb[r] = ld.tile([P, N], BF16, name="y_sb", align_bytes=64)
+            nc.sync.dma_start(out=y_sb[r][:], in_=y[P * r : P * (r + 1), :])
+
+        def load_wh(t, nh):
+            wh_raw[t, nh] = wraw.tile([P, 4, HALF], BF16, name="wh_raw", align_bytes=64)
+            nc.sync.dma_start(
+                out=wh_raw[t, nh][:],
+                in_=wh[t].rearrange("(p j) n -> p j n", j=4)[:, :, HALF * nh : HALF * (nh + 1)],
+            )
+
+        units = [(0, 0), (1, 0), (0, 1), (1, 1), (2, 0), (2, 1)]
+        load_wh(*units[0])
+        load_x(0)
+        nc.sync.dma_start(
+            out=w_codes[:].rearrange("p g n -> p (g n)").bitcast(I32).rearrange("p (g n) -> p g n", g=2),
+            in_=w_words.bitcast(I32).rearrange("g p n -> p g n"),
+        )
+        for q in range(4):
+            nc.sync.dma_start(
+                out=w_plane[32 * q : 32 * q + 4].rearrange("p g n -> p (g n)").bitcast(I32).rearrange("p (g n) -> p g n", g=2),
+                in_=w_scales.bitcast(I32)[:, 4 * q : 4 * q + 4, :].rearrange("g r n -> r g n"),
+            )
+        nc.sync.dma_start(out=gain[:], in_=g.rearrange("(p t) -> p t", t=4))
+        load_wh(*units[1])
+        load_x(1)
+        load_wh(*units[2])
+        load_wh(*units[3])
+        load_wh(*units[4])
+        load_wh(*units[5])
+        load_x(2)
+        load_oy(0)
+        load_x(3)
+        load_oy(1)
+        for r in range(2, ROWS):
+            if r + 2 < ROWS:
+                load_x(r + 2)
+            load_oy(r)
+
+        wh_il, wh_codes, wh_scales = {}, {}, {}
+        xt, xg, xq, xs, u_ps, th, ht, hb, hq, hs = ({} for _ in range(10))
+        z, a0, rr, t1, err, d, w, v, res, rb, rt, pg = ({} for _ in range(12))
+        pq, psc, qb = {}, {}, {}
+
+        def wh_interleave(t, nh, eng):
+            wh_il[t, nh] = wraw.tile([P, HALF, 4], BF16, name="wh_il", align_bytes=64)
+            src = wh_raw[t, nh][:].rearrange("p j n -> p n j")
+            dst = wh_il[t, nh][:]
+            if eng == "v":
+                nc.vector.tensor_copy(out=dst, in_=src)
+            elif eng == "s":
+                nc.scalar.copy(out=dst, in_=src)
+            else:
+                nc.gpsimd.tensor_scalar(out=dst, in0=src, scalar1=1.0, scalar2=0.0, op0=ALU.mult, op1=ALU.add)
+
+        def wh_quant(t, nh):
+            wh_codes[t, nh] = const.tile([P, HALF], U32, name="whc%d%d" % (t, nh), align_bytes=64)
+            wh_scales[t, nh] = const.tile([P, HALF], U8, name="whs%d%d" % (t, nh), align_bytes=64)
+            nc.vector.quantize_mx(
+                out=wh_codes[t, nh][:].bitcast(FP8X4),
+                scales=wh_scales[t, nh][:],
+                in_=wh_il[t, nh][:].rearrange("p n j -> p (n j)"),
+            )
+
+        def x_transpose(r):
+            xt[r] = ps_2.tile([P, 2, 2, P], F32, name="xt", tag="turn")
+            words = x_sb[r][:].bitcast(F32)
+            for gg in range(2):
+                for uu in range(2):
+                    nc.tensor.transpose(xt[r][:, gg, uu, :], words[:, 256 * gg + uu : 256 * (gg + 1) : 2], ident[:])
+
+        def x_copy(r, eng):
+            xg[r] = st.tile([P, 2, P, 4], BF16, name="xg", align_bytes=64)
+            dst = xg[r][:].rearrange("p g b t -> p (g b t)").bitcast(F32).rearrange("p (g b u) -> p g b u", g=2, u=2)
+            src = xt[r][:].rearrange("p g u b -> p g b u")
+            if eng == "s":
+                nc.scalar.copy(out=dst, in_=src)
+            else:
+                nc.vector.tensor_copy(out=dst, in_=src)
+
+        def x_quant(r):
+            xq[r] = st.tile([P, 2 * P], U32, name="xq", align_bytes=64)
+            xs[r] = st.tile([P, 2 * P], U8, name="xs", align_bytes=64)
+            nc.vector.quantize_mx(
+                out=xq[r][:].bitcast(FP8X4), scales=xs[r][:], in_=xg[r][:].rearrange("p g b t -> p (g b t)")
+            )
+
+        def trunk(r):
+            u_ps[r] = ps_1.tile([P, H], F32, name="u", tag="trunk")
+            for gg in range(2):
+                nc.tensor.matmul_mx(
+                    out=u_ps[r][:],
+                    lhsT=xq[r][:, P * gg : P * (gg + 1)].bitcast(FP8X4),
+                    lhsT_scale=xs[r][:, P * gg : P * (gg + 1)],
+                    rhs=w_codes[:, gg, :].bitcast(FP4X4),
+                    rhs_scale=w_plane[:, gg, :],
+                    start=(gg == 0),
+                    stop=(gg == 1),
+                )
+
+        def tanh(r):
+            th[r] = st.tile([P, 4, P], F32, name="th", align_bytes=64)
+            nc.scalar.activation(out=th[r][:], in_=u_ps[r][:].rearrange("b (p t) -> b t p", t=4), func=ACT.Tanh)
+
+        def h_transpose(r):
+            ht[r] = ps_1.tile([P, 4, P], F32, name="ht", tag="trunk")
+            for t in range(4):
+                nc.tensor.transpose(ht[r][:, t, :], th[r][:, t, :], ident[:])
+
+        def h_gain(r):
+            hb[r] = st.tile([P, P, 4], BF16, name="hb", align_bytes=64)
+            nc.vector.tensor_tensor(
+                out=hb[r][:],
+                in0=ht[r][:].rearrange("p t b -> p b t"),
+                in1=gain[:].unsqueeze(1).to_broadcast([P, P, 4]),
+                op=ALU.mult,
+            )
+
+        def h_quant(r):
+            hq[r] = st3.tile([P, P], U32, name="hq", align_bytes=64)
+            hs[r] = st3.tile([P, P], U8, name="hs", align_bytes=64)
+            nc.vector.quantize_mx(
+                out=hq[r][:].bitcast(FP8X4), scales=hs[r][:], in_=hb[r][:].rearrange("p b t -> p (b t)")
+            )
+
+        def head(r, nh, t):
+            if t < 2:
+                z[r, nh, t] = ps_2.tile([P, HALF], F32, name="z01")
+            else:
+                z[r, nh, t] = ps_2.tile([P, HALF], F32, name="z2")
+            if t == 1:
+                for c in range(4):
+                    k = slice(P * c, P * (c + 1))
+                    nc.tensor.matmul_mx(
+                        out=z[r, nh, t][:, k],
+                        lhsT=wh_codes[t, nh][:, k].bitcast(FP8X4),
+                        lhsT_scale=wh_scales[t, nh][:, k],
+                        rhs=hq[r][:].bitcast(FP8X4),
+                        rhs_scale=hs[r][:],
+                        start=True,
+                        stop=True,
+                    )
+                return
+            nc.tensor.matmul_mx(
+                out=z[r, nh, t][:],
+                lhsT=hq[r][:].bitcast(FP8X4),
+                lhsT_scale=hs[r][:],
+                rhs=wh_codes[t, nh][:].bitcast(FP8X4),
+                rhs_scale=wh_scales[t, nh][:],
+                start=True,
+                stop=True,
+            )
+
+        def cols(nh):
+            return slice(HALF * nh, HALF * (nh + 1))
+
+        def get(store, r, name, dt=F32):
+            if r not in store:
+                store[r] = st.tile([P, N], dt, name=name, align_bytes=64)
+            return store[r]
+
+        def exp0(r, nh):
+            nc.scalar.activation(out=get(a0, r, "a0")[:, cols(nh)], in_=z[r, nh, 0][:], func=ACT.Exp, scale=-1.0)
+
+        def tanh1(r, nh):
+            nc.scalar.activation(out=get(t1, r, "t1")[:, cols(nh)], in_=z[r, nh, 1][:], func=ACT.Tanh, scale=0.5)
+
+        def subtract(r, nh):
+            q = qb[r, nh] = ps_1.tile([P, HALF], F32, name="qb")
+            nc.tensor.matmul(q[:], lhsT=minus2[:], rhs=y_sb[r][:, cols(nh)], start=True, stop=False)
+            for c in range(4):
+                k = slice(P * c, P * (c + 1))
+                nc.tensor.matmul(
+                    q[:, k], lhsT=t1[r][:, HALF * nh + P * c : HALF * nh + P * (c + 1)], rhs=ident[:],
+                    is_transpose=True, start=False, stop=(c == 3),
+                )
+
+        def square(r, nh):
+            nc.scalar.activation(out=get(err, r, "err")[:, cols(nh)], in_=qb[r, nh][:], func=ACT.Square, scale=0.5, bias=0.5)
+
+        def inv_p(r, nh, eng="g"):
+            get(rr, r, "rr")
+            e = nc.gpsimd if eng == "g" else nc.vector
+            e.tensor_scalar(out=rr[r][:, cols(nh)], in0=a0[r][:, cols(nh)], scalar1=1.0, scalar2=5.0, op0=ALU.add, op1=ALU.min)
+
+        def weight(r, nh, eng="v"):
+            c = cols(nh)
+            get(w, r, "w")
+            e = nc.gpsimd if eng == "g" else nc.vector
+            e.tensor_tensor(out=w[r][:, c], in0=rr[r][:, c], in1=o_sb[r][:, c], op=ALU.mult)
+
+        def diff(r, nh):
+            c = cols(nh)
+            get(d, r, "d")
+            nc.vector.tensor_tensor(out=d[r][:, c], in0=err[r][:, c], in1=z[r, nh, 2][:], op=ALU.subtract)
+
+        def prod(r, nh):
+            c = cols(nh)
+            get(v, r, "v")
+            nc.vector.tensor_tensor(out=v[r][:, c], in0=w[r][:, c], in1=d[r][:, c], op=ALU.mult)
+
+        def result(r, nh):
+            c = cols(nh)
+            get(res, r, "res")
+            nc.vector.tensor_tensor(out=res[r][:, c], in0=z[r, nh, 2][:], in1=v[r][:, c], op=ALU.add)
+
+        def store_r(r, nh):
+            c = cols(nh)
+            nc.sync.dma_start(out=out_0[P * r : P * (r + 1), c], in_=res[r][:, c])
+
+        def round_r(r, nh, eng):
+            get(rb, r, "rb", BF16)
+            c = cols(nh)
+            dst = rb[r][:, c].rearrange("b (u p e) -> b u p e", u=2, e=2)
+            src = res[r][:, c].rearrange("b (p u e) -> b u p e", u=2, e=2)
+            if eng == "s":
+                nc.scalar.copy(out=dst, in_=src)
+            else:
+                nc.vector.tensor_copy(out=dst, in_=src)
+
+        def r_transpose(r):
+            rt[r] = ps_2.tile([P, 2, 2, P], F32, name="rt", tag="turn")
+            words = rb[r][:].bitcast(F32)
+            for gg in range(2):
+                for uu in range(2):
+                    nc.tensor.transpose(rt[r][:, gg, uu, :], words[:, 256 * gg + P * uu : 256 * gg + P * (uu + 1)], ident[:])
+
+        def r_copy(r):
+            pg[r] = st.tile([P, 2, P, 4], BF16, name="pg", align_bytes=64)
+            nc.scalar.copy(
+                out=pg[r][:].rearrange("p g b t -> p (g b t)").bitcast(F32).rearrange("p (g b u) -> p g b u", g=2, u=2),
+                in_=rt[r][:].rearrange("p g u b -> p g b u"),
+            )
+
+        def r_quant(r):
+            hf, k = r // 4, r % 4
+            if k == 0:
+                pq[hf] = st.tile([P, 2, HALF], U32, name="pq", align_bytes=64)
+                psc[hf] = st.tile([P, 2, HALF], U8, name="psc", align_bytes=64)
+            for gg in range(2):
+                nc.vector.quantize_mx(
+                    out=pq[hf][:, gg, P * k : P * (k + 1)].bitcast(FP8X4),
+                    scales=psc[hf][:, gg, P * k : P * (k + 1)],
+                    in_=pg[r][:, gg, :, :].rearrange("p b t -> p (b t)"),
+                )
+
+        def store_planes(r):
+            hf, k = r // 4, r % 4
+            nc.sync.dma_start(
+                out=out_1.rearrange("g p m t -> p g (m t)").bitcast(I32)[:, :, P * r : P * (r + 1)],
+                in_=pq[hf][:, :, P * k : P * (k + 1)].bitcast(I32),
+            )
+            if k == 3:
+                for q in range(4):
+                    nc.sync.dma_start(
+                        out=out_2.bitcast(I32)[:, 4 * q : 4 * q + 4, P * hf : P * (hf + 1)].rearrange("g r m -> r g m"),
+                        in_=psc[hf][32 * q : 32 * q + 4].rearrange("p g m -> p (g m)").bitcast(I32).rearrange("p (g m) -> p g m", g=2),
+                    )
+
+        def ok(r):
+            return 0 <= r < ROWS
+
+        with tc.manual_schedule():
+            wh_interleave(*units[0], "v")
+            x_transpose(0)
+            x_copy(0, "s")
+            wh_quant(*units[0])
+            x_quant(0)
+            x_transpose(1)
+            trunk(0)
+            tanh(0)
+            wh_interleave(*units[1], "v")
+            wh_quant(*units[1])
+            h_transpose(0)
+            x_copy(1, "s")
+            h_gain(0)
+            x_quant(1)
+            wh_interleave(*units[2], "s")
+            trunk(1)
+            wh_interleave(*units[3], "v")
+            tanh(1)
+            wh_interleave(*units[5], "s")
+            x_transpose(2)
+            h_quant(0)
+            h_transpose(1)
+            wh_interleave(*units[4], "v")
+            wh_quant(*units[3])
+            head(0, 0, 0)
+            wh_quant(*units[4])
+            h_gain(1)
+            x_copy(2, "s")
+            wh_quant(*units[2])
+            x_quant(2)
+            wh_quant(*units[5])
+            for s in range(0, ROWS + 4):
+                if ok(s):
+                    exp0(s, 0)
+                if ok(s):
+                    head(s, 0, 1)
+                if ok(s - 3):
+                    r_quant(s - 3)
+                if ok(s - 1):
+                    prod(s - 1, 1)
+                if ok(s):
+                    tanh1(s, 0)
+                if ok(s + 2):
+                    trunk(s + 2)
+                if ok(s):
+                    head(s, 1, 0)
+                if ok(s + 2):
+                    tanh(s + 2)
+                if ok(s):
+                    subtract(s, 0)
+                if ok(s):
+                    exp0(s, 1)
+                if ok(s - 1):
+                    result(s - 1, 0)
+                if ok(s + 2):
+                    h_transpose(s + 2)
+                if ok(s):
+                    head(s, 1, 1)
+                if ok(s):
+                    square(s, 0)
+                if ok(s - 2):
+                    round_r(s - 2, 1, "v")
+                if ok(s):
+                    inv_p(s, 0)
+                if ok(s):
+                    head(s, 0, 2)
+                if ok(s):
+                    weight(s, 0)
+                if ok(s - 4):
+                    store_planes(s - 4)
+                if ok(s - 2):
+                    r_transpose(s - 2)
+                if ok(s + 2):
+                    h_gain(s + 2)
+                if ok(s):
+                    tanh1(s, 1)
+                if ok(s):
+                    inv_p(s, 1)
+                if ok(s - 1):
+                    round_r(s - 1, 0, "s")
+                if ok(s):
+                    subtract(s, 1)
+                if ok(s):
+                    diff(s, 0)
+                if ok(s):
+                    square(s, 1)
+                if ok(s - 1):
+                    result(s - 1, 1)
+                if ok(s + 3):
+                    x_transpose(s + 3)
+                if ok(s):
+                    weight(s, 1, "g")
+                if ok(s):
+                    head(s, 1, 2)
+                if ok(s + 3):
+                    x_copy(s + 3, "s")
+                if ok(s):
+                    prod(s, 0)
+                if ok(s + 1):
+                    h_quant(s + 1)
+                if ok(s):
+                    diff(s, 1)
+                if ok(s + 3):
+                    x_quant(s + 3)
+                if ok(s - 2):
+                    r_copy(s - 2)
+                if ok(s + 1):
+                    head(s + 1, 0, 0)
+                if ok(s - 2):
+                    store_r(s - 2, 1)
+                if ok(s - 2):
+                    store_r(s - 2, 0)

@@ -321,109 +321,117 @@ def tile_escmdoublyrobusterrormap_x2_kernel(tc, x, w_words, w_scales, g, wh, o, 
             wh_quant(*units[0])
             x_quant(0)
             x_transpose(1)
-            trunk(0)
-            tanh(0)
             wh_interleave(*units[1], "v")
-            wh_quant(*units[1])
+            trunk(0)
+            wh_interleave(*units[2], "v")
+            tanh(0)
             h_transpose(0)
-            x_copy(1, "s")
             h_gain(0)
+            x_copy(1, "s")
             x_quant(1)
-            wh_interleave(*units[2], "s")
-            trunk(1)
-            wh_interleave(*units[3], "v")
-            tanh(1)
             wh_interleave(*units[5], "s")
+            trunk(1)
             x_transpose(2)
             h_quant(0)
+            tanh(1)
+            wh_interleave(*units[3], "v")
+            wh_quant(*units[2])
+            head(0, 0, 0)
+            wh_quant(*units[3])
             h_transpose(1)
             wh_interleave(*units[4], "v")
-            wh_quant(*units[3])
-            head(0, 0, 0)
-            wh_quant(*units[4])
-            h_gain(1)
             x_copy(2, "s")
-            wh_quant(*units[2])
+            wh_quant(*units[1])
+            exp0(0, 0)
+            h_gain(1)
             x_quant(2)
+            h_quant(1)
+            inv_p(0, 0, "v")
+            wh_quant(*units[4])
+            head(0, 1, 0)
+            head(0, 0, 1)
+            exp0(0, 1)
+            tanh1(0, 0)
             wh_quant(*units[5])
+            trunk(2)
             for s in range(0, ROWS + 4):
+                if ok(s - 2):
+                    r_copy(s - 2)
                 if ok(s):
-                    exp0(s, 0)
-                if ok(s):
-                    head(s, 0, 1)
-                if ok(s - 3):
-                    r_quant(s - 3)
-                if ok(s - 1):
-                    prod(s - 1, 1)
-                if ok(s):
-                    tanh1(s, 0)
-                if ok(s + 2):
-                    trunk(s + 2)
-                if ok(s):
-                    head(s, 1, 0)
-                if ok(s + 2):
-                    tanh(s + 2)
+                    inv_p(s, 1, "v")
                 if ok(s):
                     subtract(s, 0)
                 if ok(s):
-                    exp0(s, 1)
-                if ok(s - 1):
-                    result(s - 1, 0)
-                if ok(s + 2):
-                    h_transpose(s + 2)
-                if ok(s):
-                    head(s, 1, 1)
-                if ok(s):
-                    square(s, 0)
-                if ok(s - 2):
-                    round_r(s - 2, 1, "v")
-                if ok(s):
-                    inv_p(s, 0)
+                    weight(s, 0, "v")
                 if ok(s):
                     head(s, 0, 2)
-                if ok(s):
-                    weight(s, 0)
-                if ok(s - 4):
-                    store_planes(s - 4)
                 if ok(s - 2):
-                    r_transpose(s - 2)
-                if ok(s + 2):
-                    h_gain(s + 2)
-                if ok(s):
-                    tanh1(s, 1)
-                if ok(s):
-                    inv_p(s, 1)
+                    r_quant(s - 2)
+                if ok(s - 2):
+                    store_r(s - 2, 0)
                 if ok(s - 1):
                     round_r(s - 1, 0, "s")
+                if ok(s + 2):
+                    tanh(s + 2)
+                if ok(s - 1):
+                    prod(s - 1, 1)
                 if ok(s):
-                    subtract(s, 1)
+                    square(s, 0)
                 if ok(s):
                     diff(s, 0)
+                if ok(s + 1):
+                    head(s + 1, 0, 0)
                 if ok(s):
-                    square(s, 1)
+                    head(s, 1, 1)
+                if ok(s + 2):
+                    h_transpose(s + 2)
+                if ok(s + 1):
+                    exp0(s + 1, 0)
                 if ok(s - 1):
                     result(s - 1, 1)
+                if ok(s + 2):
+                    h_gain(s + 2)
+                if ok(s - 2):
+                    store_r(s - 2, 1)
+                if ok(s):
+                    tanh1(s, 1)
                 if ok(s + 3):
                     x_transpose(s + 3)
-                if ok(s):
-                    weight(s, 1, "g")
-                if ok(s):
-                    head(s, 1, 2)
                 if ok(s + 3):
                     x_copy(s + 3, "s")
                 if ok(s):
                     prod(s, 0)
-                if ok(s + 1):
-                    h_quant(s + 1)
                 if ok(s):
-                    diff(s, 1)
+                    subtract(s, 1)
+                if ok(s + 1):
+                    head(s + 1, 0, 1)
+                if ok(s + 1):
+                    head(s + 1, 1, 0)
+                if ok(s + 2):
+                    h_quant(s + 2)
+                if ok(s - 2):
+                    store_planes(s - 2)
                 if ok(s + 3):
                     x_quant(s + 3)
-                if ok(s - 2):
-                    r_copy(s - 2)
+                if ok(s):
+                    weight(s, 1, "v")
+                if ok(s):
+                    result(s, 0)
+                if ok(s - 1):
+                    round_r(s - 1, 1, "s")
+                if ok(s):
+                    square(s, 1)
+                if ok(s):
+                    head(s, 1, 2)
+                if ok(s + 3):
+                    trunk(s + 3)
                 if ok(s + 1):
-                    head(s + 1, 0, 0)
-                if ok(s - 2):
-                    store_r(s - 2, 1)
-                if ok(s - 2):
-                    store_r(s - 2, 0)
+                    inv_p(s + 1, 0, "v")
+                if ok(s + 1):
+                    exp0(s + 1, 1)
+                if ok(s - 1):
+                    r_transpose(s - 1)
+                if ok(s + 1):
+                    tanh1(s + 1, 0)
+                if ok(s):
+                    diff(s, 1)

@@ -98,8 +98,8 @@ def tile_escmdoublyrobusterrormap_x2_kernel(tc, x, w_words, w_scales, g, wh, o, 
 
         def wh_interleave(t, nh, eng):
             wh_il[t, nh] = wraw.tile([P, HALF, 4], BF16, name="wh_il", align_bytes=64)
-            src = wh_raw[t, nh][:].rearrange("p j n -> p n j")
-            dst = wh_il[t, nh][:]
+            src = wh_raw[t, nh][:].rearrange("p j (c i) -> p c j i", i=4)
+            dst = wh_il[t, nh][:].rearrange("p (c i) j -> p c j i", i=4)
             if eng == "v":
                 nc.vector.tensor_copy(out=dst, in_=src)
             elif eng == "s":
@@ -232,12 +232,23 @@ def tile_escmdoublyrobusterrormap_x2_kernel(tc, x, w_words, w_scales, g, wh, o, 
         def square(r, nh):
             nc.scalar.activation(out=get(err, r, "err")[:, cols(nh)], in_=qb[r, nh][:], func=ACT.Square, scale=0.5, bias=0.5)
 
-        def inv_p(r, nh, eng="g"):
+        def inv_p(r):
             get(rr, r, "rr")
-            e = nc.gpsimd if eng == "g" else nc.vector
-            e.tensor_scalar(out=rr[r][:, cols(nh)], in0=a0[r][:, cols(nh)], scalar1=1.0, scalar2=5.0, op0=ALU.add, op1=ALU.min)
+            nc.vector.tensor_scalar(out=rr[r][:], in0=a0[r][:], scalar1=1.0, scalar2=5.0, op0=ALU.add, op1=ALU.min)
 
-        def weight(r, nh, eng="v"):
+        def inv_half(r, nh):
+            c = cols(nh)
+            get(rr, r, "rr")
+            nc.vector.tensor_scalar(
+                out=rr[r][:, c], in0=a0[r][:, c], scalar1=1.0, scalar2=5.0, op0=ALU.add, op1=ALU.min
+            )
+
+        def weight(r, eng="v"):
+            get(w, r, "w")
+            e = nc.gpsimd if eng == "g" else nc.vector
+            e.tensor_tensor(out=w[r][:], in0=rr[r][:], in1=o_sb[r][:], op=ALU.mult)
+
+        def weight_half(r, nh, eng):
             c = cols(nh)
             get(w, r, "w")
             e = nc.gpsimd if eng == "g" else nc.vector
@@ -248,8 +259,8 @@ def tile_escmdoublyrobusterrormap_x2_kernel(tc, x, w_words, w_scales, g, wh, o, 
             get(d, r, "d")
             nc.vector.tensor_tensor(out=d[r][:, c], in0=err[r][:, c], in1=z[r, nh, 2][:], op=ALU.subtract)
 
-        def prod(r, nh):
-            c = cols(nh)
+        def prod(r, nh=None):
+            c = slice(0, N) if nh is None else cols(nh)
             get(v, r, "v")
             nc.vector.tensor_tensor(out=v[r][:, c], in0=w[r][:, c], in1=d[r][:, c], op=ALU.mult)
 
@@ -262,176 +273,281 @@ def tile_escmdoublyrobusterrormap_x2_kernel(tc, x, w_words, w_scales, g, wh, o, 
             c = cols(nh)
             nc.sync.dma_start(out=out_0[P * r : P * (r + 1), c], in_=res[r][:, c])
 
-        def round_r(r, nh, eng):
+        def round_r(r, eng, nh=None):
             get(rb, r, "rb", BF16)
-            c = cols(nh)
-            dst = rb[r][:, c].rearrange("b (u p e) -> b u p e", u=2, e=2)
-            src = res[r][:, c].rearrange("b (p u e) -> b u p e", u=2, e=2)
+            c = slice(0, N) if nh is None else cols(nh)
+            k = 2 if nh is None else 1
+            dst = rb[r][:, c].rearrange("b (h u p e) -> b h u p e", h=k, u=2, e=2)
+            src = res[r][:, c].rearrange("b (h p u e) -> b h u p e", h=k, u=2, e=2)
+            for h in range(k):
+                if eng == "s":
+                    nc.scalar.copy(out=dst[:, h], in_=src[:, h])
+                else:
+                    nc.vector.tensor_copy(out=dst[:, h], in_=src[:, h])
+
+        def r_transpose(r, nh=None):
+            if r not in rt:
+                rt[r] = ps_2.tile([P, 2, 2, P], F32, name="rt", tag="turn")
+            words = rb[r][:].bitcast(F32)
+            for gg in range(2) if nh is None else (nh,):
+                for uu in range(2):
+                    k = 256 * gg + P * uu
+                    nc.tensor.transpose(rt[r][:, gg, uu, :], words[:, k : k + P], ident[:])
+
+        def r_copy(r, eng="s", nh=None):
+            pair, k = r // 2, r % 2
+            if pair not in pg:
+                pg[pair] = st.tile([P, 2, 2 * P, 4], BF16, name="pg", align_bytes=64)
+            words = pg[pair][:].rearrange("p g b t -> p (g b t)").bitcast(F32).rearrange("p (g b u) -> p g b u", g=2, u=2)
+            h = slice(0, 2) if nh is None else slice(nh, nh + 1)
+            dst = words[:, h, P * k : P * (k + 1), :]
+            src = rt[r][:, h].rearrange("p g u b -> p g b u")
             if eng == "s":
                 nc.scalar.copy(out=dst, in_=src)
             else:
                 nc.vector.tensor_copy(out=dst, in_=src)
 
-        def r_transpose(r):
-            rt[r] = ps_2.tile([P, 2, 2, P], F32, name="rt", tag="turn")
-            words = rb[r][:].bitcast(F32)
-            for gg in range(2):
-                for uu in range(2):
-                    nc.tensor.transpose(rt[r][:, gg, uu, :], words[:, 256 * gg + P * uu : 256 * gg + P * (uu + 1)], ident[:])
-
-        def r_copy(r):
-            pg[r] = st.tile([P, 2, P, 4], BF16, name="pg", align_bytes=64)
-            nc.scalar.copy(
-                out=pg[r][:].rearrange("p g b t -> p (g b t)").bitcast(F32).rearrange("p (g b u) -> p g b u", g=2, u=2),
-                in_=rt[r][:].rearrange("p g u b -> p g b u"),
-            )
-
-        def r_quant(r):
-            hf, k = r // 4, r % 4
-            if k == 0:
-                pq[hf] = st.tile([P, 2, HALF], U32, name="pq", align_bytes=64)
-                psc[hf] = st.tile([P, 2, HALF], U8, name="psc", align_bytes=64)
-            for gg in range(2):
+        def r_quant(pair, k=None, nh=None):
+            if pair not in pq:
+                pq[pair] = st.tile([P, 2, 2 * P], U32, name="pq", align_bytes=64)
+                psc[pair] = st.tile([P, 2, 2 * P], U8, name="psc", align_bytes=64)
+            if k is None:
                 nc.vector.quantize_mx(
-                    out=pq[hf][:, gg, P * k : P * (k + 1)].bitcast(FP8X4),
-                    scales=psc[hf][:, gg, P * k : P * (k + 1)],
-                    in_=pg[r][:, gg, :, :].rearrange("p b t -> p (b t)"),
+                    out=pq[pair][:].rearrange("p g m -> p (g m)").bitcast(FP8X4),
+                    scales=psc[pair][:].rearrange("p g m -> p (g m)"),
+                    in_=pg[pair][:].rearrange("p g b t -> p (g b t)"),
                 )
-
-        def store_planes(r):
-            hf, k = r // 4, r % 4
-            nc.sync.dma_start(
-                out=out_1.rearrange("g p m t -> p g (m t)").bitcast(I32)[:, :, P * r : P * (r + 1)],
-                in_=pq[hf][:, :, P * k : P * (k + 1)].bitcast(I32),
+                return
+            m = slice(P * k, P * (k + 1))
+            nc.vector.quantize_mx(
+                out=pq[pair][:, nh, m].bitcast(FP8X4),
+                scales=psc[pair][:, nh, m],
+                in_=pg[pair][:, nh, m, :].rearrange("p b t -> p (b t)"),
             )
-            if k == 3:
-                for q in range(4):
-                    nc.sync.dma_start(
-                        out=out_2.bitcast(I32)[:, 4 * q : 4 * q + 4, P * hf : P * (hf + 1)].rearrange("g r m -> r g m"),
-                        in_=psc[hf][32 * q : 32 * q + 4].rearrange("p g m -> p (g m)").bitcast(I32).rearrange("p (g m) -> p g m", g=2),
-                    )
+
+        def store_words(pair, k=None):
+            lo, hi = (0, 2 * P) if k is None else (P * k, P * (k + 1))
+            nc.sync.dma_start(
+                out=out_1.rearrange("g p m t -> p g (m t)").bitcast(I32)[:, :, 2 * P * pair + lo : 2 * P * pair + hi],
+                in_=pq[pair][:, :, lo:hi].bitcast(I32),
+            )
+
+        def store_scales(pair):
+            for q in range(4):
+                nc.sync.dma_start(
+                    out=out_2.bitcast(I32)[:, 4 * q : 4 * q + 4, 64 * pair : 64 * (pair + 1)].rearrange("g r m -> r g m"),
+                    in_=psc[pair][32 * q : 32 * q + 4].rearrange("p g m -> p (g m)").bitcast(I32).rearrange("p (g m) -> p g m", g=2),
+                )
 
         def ok(r):
             return 0 <= r < ROWS
 
         with tc.manual_schedule():
-            wh_interleave(*units[0], "v")
             x_transpose(0)
-            x_copy(0, "s")
+            wh_interleave(*units[0], "v")
+            x_copy(0, "v")
             wh_quant(*units[0])
             x_quant(0)
+            trunk(0)
             x_transpose(1)
             wh_interleave(*units[1], "v")
-            trunk(0)
+            x_copy(1, "s")
             wh_interleave(*units[2], "v")
             tanh(0)
+            wh_quant(*units[1])
             h_transpose(0)
             h_gain(0)
-            x_copy(1, "s")
+            wh_interleave(*units[3], "s")
             x_quant(1)
-            wh_interleave(*units[5], "s")
-            trunk(1)
-            x_transpose(2)
             h_quant(0)
-            tanh(1)
-            wh_interleave(*units[3], "v")
-            wh_quant(*units[2])
-            head(0, 0, 0)
+            wh_interleave(*units[5], "v")
+            trunk(1)
+            head(0, 0, 1)
             wh_quant(*units[3])
+            wh_quant(*units[5])
+            tanh(1)
+            x_transpose(2)
+            tanh1(0, 0)
             h_transpose(1)
-            wh_interleave(*units[4], "v")
+            head(0, 1, 1)
+            subtract(0, 0)
+            x_transpose(3)
             x_copy(2, "s")
-            wh_quant(*units[1])
-            exp0(0, 0)
             h_gain(1)
             x_quant(2)
-            h_quant(1)
-            inv_p(0, 0, "v")
-            wh_quant(*units[4])
-            head(0, 1, 0)
-            head(0, 0, 1)
-            exp0(0, 1)
-            tanh1(0, 0)
-            wh_quant(*units[5])
             trunk(2)
-            for s in range(0, ROWS + 4):
+            square(0, 0)
+            wh_interleave(*units[4], "v")
+            h_quant(1)
+            tanh1(0, 1)
+            wh_quant(*units[2])
+            head(0, 1, 2)
+            wh_quant(*units[4])
+            head(0, 0, 0)
+            tanh(2)
+            exp0(0, 0)
+            subtract(0, 1)
+            inv_half(0, 0)
+            h_transpose(2)
+            weight_half(0, 0, "g")
+            x_copy(3, "s")
+            square(0, 1)
+            head(0, 1, 0)
+            head(1, 0, 1)
+            x_transpose(5)
+            x_transpose(4)
+            exp0(0, 1)
+            x_quant(3)
+            h_gain(2)
+            tanh1(1, 0)
+            diff(0, 1)
+            head(1, 1, 0)
+            exp0(1, 1)
+            head(0, 0, 2)
+            inv_half(0, 1)
+            h_quant(2)
+            x_copy(5, "v")
+            trunk(3)
+            diff(0, 0)
+            x_copy(4, "s")
+            weight_half(0, 1, "g")
+            head(1, 1, 1)
+            x_quant(4)
+            prod(0)
+            tanh1(1, 1)
+            subtract(1, 0)
+            for s in range(1, 6):
+                if ok(s + 5):
+                    x_transpose(s + 5)
                 if ok(s - 2):
-                    r_copy(s - 2)
-                if ok(s):
-                    inv_p(s, 1, "v")
-                if ok(s):
-                    subtract(s, 0)
-                if ok(s):
-                    weight(s, 0, "v")
-                if ok(s):
-                    head(s, 0, 2)
+                    round_r(s - 2, "v", 0)
+                square(s, 0)
+                head(s + 1, 0, 1)
+                head(s, 0, 0)
+                inv_half(s, 1)
+                if (s - 4) % 2 == 1 and s - 4 > 0:
+                    r_quant((s - 4) // 2)
+                tanh(s + 2)
+                subtract(s, 1)
+                if ok(s + 4):
+                    x_quant(s + 4)
+                tanh1(s + 1, 0)
+                weight_half(s, 1, "g")
+                result(s - 1, 1)
+                if ok(s - 3):
+                    r_transpose(s - 3)
+                exp0(s, 0)
+                result(s - 1, 0)
+                h_transpose(s + 2)
+                inv_half(s, 0)
+                head(s + 1, 1, 1)
+                head(s + 1, 1, 0)
                 if ok(s - 2):
-                    r_quant(s - 2)
-                if ok(s - 2):
-                    store_r(s - 2, 0)
-                if ok(s - 1):
-                    round_r(s - 1, 0, "s")
-                if ok(s + 2):
-                    tanh(s + 2)
-                if ok(s - 1):
-                    prod(s - 1, 1)
-                if ok(s):
-                    square(s, 0)
-                if ok(s):
-                    diff(s, 0)
-                if ok(s + 1):
-                    head(s + 1, 0, 0)
-                if ok(s):
-                    head(s, 1, 1)
-                if ok(s + 2):
-                    h_transpose(s + 2)
-                if ok(s + 1):
-                    exp0(s + 1, 0)
-                if ok(s - 1):
-                    result(s - 1, 1)
-                if ok(s + 2):
-                    h_gain(s + 2)
+                    round_r(s - 2, "s", 1)
+                head(s, 0, 2)
+                square(s, 1)
+                h_gain(s + 2)
+                if (s - 4) % 2 == 1 and s - 4 > 0:
+                    store_scales((s - 4) // 2)
+                head(s, 1, 2)
+                if ok(s + 5):
+                    x_copy(s + 5, "s")
+                diff(s, 0)
+                if (s - 4) % 2 == 1 and s - 4 > 0:
+                    store_words((s - 4) // 2)
+                diff(s, 1)
+                h_quant(s + 2)
+                exp0(s + 1, 1)
+                weight_half(s, 0, "g")
+                subtract(s + 1, 0)
                 if ok(s - 2):
                     store_r(s - 2, 1)
-                if ok(s):
-                    tanh1(s, 1)
-                if ok(s + 3):
-                    x_transpose(s + 3)
-                if ok(s + 3):
-                    x_copy(s + 3, "s")
-                if ok(s):
-                    prod(s, 0)
-                if ok(s):
-                    subtract(s, 1)
-                if ok(s + 1):
-                    head(s + 1, 0, 1)
-                if ok(s + 1):
-                    head(s + 1, 1, 0)
-                if ok(s + 2):
-                    h_quant(s + 2)
-                if ok(s - 2):
-                    store_planes(s - 2)
-                if ok(s + 3):
-                    x_quant(s + 3)
-                if ok(s):
-                    weight(s, 1, "v")
-                if ok(s):
-                    result(s, 0)
-                if ok(s - 1):
-                    round_r(s - 1, 1, "s")
-                if ok(s):
-                    square(s, 1)
-                if ok(s):
-                    head(s, 1, 2)
+                prod(s)
+                if ok(s - 3):
+                    r_copy(s - 3, "s")
+                tanh1(s + 1, 1)
                 if ok(s + 3):
                     trunk(s + 3)
-                if ok(s + 1):
-                    inv_p(s + 1, 0, "v")
-                if ok(s + 1):
-                    exp0(s + 1, 1)
-                if ok(s - 1):
-                    r_transpose(s - 1)
-                if ok(s + 1):
-                    tanh1(s + 1, 0)
-                if ok(s):
-                    diff(s, 1)
+                store_r(s - 1, 0)
+            square(6, 0)
+            head(6, 0, 0)
+            store_r(4, 1)
+            exp0(6, 0)
+            subtract(6, 1)
+            inv_half(6, 0)
+            head(7, 0, 1)
+            r_transpose(3)
+            inv_half(6, 1)
+            result(5, 0)
+            round_r(4, "s", 0)
+            round_r(4, "s", 1)
+            head(6, 0, 2)
+            square(6, 1)
+            tanh1(7, 0)
+            result(5, 1)
+            head(7, 0, 0)
+            r_copy(3, "s")
+            head(6, 1, 2)
+            diff(6, 0)
+            subtract(7, 0)
+            diff(6, 1)
+            r_quant(1)
+            store_scales(1)
+            weight_half(6, 0, "g")
+            exp0(7, 0)
+            head(7, 1, 0)
+            square(7, 0)
+            head(7, 1, 1)
+            round_r(5, "s", 0)
+            tanh1(7, 1)
+            subtract(7, 1)
+            weight_half(6, 1, "g")
+            prod(6)
+            exp0(7, 1)
+            inv_half(7, 0)
+            store_r(5, 1)
+            result(6, 0)
+            round_r(5, "s", 1)
+            r_transpose(4)
+            head(7, 0, 2)
+            result(6, 1)
+            weight_half(7, 0, "g")
+            inv_half(7, 1)
+            square(7, 1)
+            head(7, 1, 2)
+            round_r(6, "s", 1)
+            store_words(1)
+            diff(7, 0)
+            round_r(6, "s", 0)
+            diff(7, 1)
+            r_copy(4, "s")
+            weight_half(7, 1, "g")
+            prod(7, 1)
+            r_transpose(5)
+            r_transpose(6)
+            store_r(5, 0)
+            r_copy(5, "s")
+            prod(7, 0)
+            r_copy(6, "s")
+            result(7, 1)
+            store_r(6, 1)
+            result(7, 0)
+            r_quant(2)
+            round_r(7, "s", 1)
+            store_r(6, 0)
+            r_quant(3, 0, 1)
+            store_r(7, 1)
+            store_r(7, 0)
+            round_r(7, "s", 0)
+            r_transpose(7, 1)
+            r_quant(3, 0, 0)
+            r_copy(7, "s", 1)
+            store_words(2)
+            r_transpose(7, 0)
+            store_words(3, 0)
+            store_scales(2)
+            r_copy(7, "v", 0)
+            r_quant(3, 1, 1)
+            r_quant(3, 1, 0)
+            store_words(3, 1)
+            store_scales(3)

@@ -93,7 +93,7 @@ def tile_escmdoublyrobusterrormap_x2_kernel(tc, x, w_words, w_scales, g, wh, o, 
 
         wh_il, wh_codes, wh_scales = {}, {}, {}
         xt, xg, xq, xs, u_ps, th, ht, hb, hq, hs = ({} for _ in range(10))
-        z, a0, rr, t1, err, d, w, v, res, rb, rt, pg = ({} for _ in range(12))
+        z, a0, t1, err, d, res, rb, rt, pg = ({} for _ in range(9))
         pq, psc, qb = {}, {}, {}
 
         def wh_interleave(t, nh, eng):
@@ -210,7 +210,7 @@ def tile_escmdoublyrobusterrormap_x2_kernel(tc, x, w_words, w_scales, g, wh, o, 
 
         def get(store, r, name, dt=F32):
             if r not in store:
-                store[r] = st.tile([P, N], dt, name=name, align_bytes=64)
+                store[r] = st3.tile([P, N], dt, name=name, align_bytes=64)
             return store[r]
 
         def exp0(r, nh):
@@ -233,26 +233,22 @@ def tile_escmdoublyrobusterrormap_x2_kernel(tc, x, w_words, w_scales, g, wh, o, 
             nc.scalar.activation(out=get(err, r, "err")[:, cols(nh)], in_=qb[r, nh][:], func=ACT.Square, scale=0.5, bias=0.5)
 
         def inv_p(r):
-            get(rr, r, "rr")
-            nc.vector.tensor_scalar(out=rr[r][:], in0=a0[r][:], scalar1=1.0, scalar2=5.0, op0=ALU.add, op1=ALU.min)
+            nc.vector.tensor_scalar(out=a0[r][:], in0=a0[r][:], scalar1=1.0, scalar2=5.0, op0=ALU.add, op1=ALU.min)
 
         def inv_half(r, nh):
             c = cols(nh)
-            get(rr, r, "rr")
             nc.vector.tensor_scalar(
-                out=rr[r][:, c], in0=a0[r][:, c], scalar1=1.0, scalar2=5.0, op0=ALU.add, op1=ALU.min
+                out=a0[r][:, c], in0=a0[r][:, c], scalar1=1.0, scalar2=5.0, op0=ALU.add, op1=ALU.min
             )
 
         def weight(r, eng="v"):
-            get(w, r, "w")
             e = nc.gpsimd if eng == "g" else nc.vector
-            e.tensor_tensor(out=w[r][:], in0=rr[r][:], in1=o_sb[r][:], op=ALU.mult)
+            e.tensor_tensor(out=a0[r][:], in0=a0[r][:], in1=o_sb[r][:], op=ALU.mult)
 
         def weight_half(r, nh, eng):
             c = cols(nh)
-            get(w, r, "w")
             e = nc.gpsimd if eng == "g" else nc.vector
-            e.tensor_tensor(out=w[r][:, c], in0=rr[r][:, c], in1=o_sb[r][:, c], op=ALU.mult)
+            e.tensor_tensor(out=a0[r][:, c], in0=a0[r][:, c], in1=o_sb[r][:, c], op=ALU.mult)
 
         def diff(r, nh):
             c = cols(nh)
@@ -261,13 +257,12 @@ def tile_escmdoublyrobusterrormap_x2_kernel(tc, x, w_words, w_scales, g, wh, o, 
 
         def prod(r, nh=None):
             c = slice(0, N) if nh is None else cols(nh)
-            get(v, r, "v")
-            nc.vector.tensor_tensor(out=v[r][:, c], in0=w[r][:, c], in1=d[r][:, c], op=ALU.mult)
+            nc.vector.tensor_tensor(out=d[r][:, c], in0=a0[r][:, c], in1=d[r][:, c], op=ALU.mult)
 
         def result(r, nh):
             c = cols(nh)
             get(res, r, "res")
-            nc.vector.tensor_tensor(out=res[r][:, c], in0=z[r, nh, 2][:], in1=v[r][:, c], op=ALU.add)
+            nc.vector.tensor_tensor(out=res[r][:, c], in0=z[r, nh, 2][:], in1=d[r][:, c], op=ALU.add)
 
         def store_r(r, nh):
             c = cols(nh)
@@ -276,14 +271,15 @@ def tile_escmdoublyrobusterrormap_x2_kernel(tc, x, w_words, w_scales, g, wh, o, 
         def round_r(r, eng, nh=None):
             get(rb, r, "rb", BF16)
             c = slice(0, N) if nh is None else cols(nh)
-            k = 2 if nh is None else 1
-            dst = rb[r][:, c].rearrange("b (h u p e) -> b h u p e", h=k, u=2, e=2)
-            src = res[r][:, c].rearrange("b (h p u e) -> b h u p e", h=k, u=2, e=2)
-            for h in range(k):
-                if eng == "s":
-                    nc.scalar.copy(out=dst[:, h], in_=src[:, h])
-                else:
-                    nc.vector.tensor_copy(out=dst[:, h], in_=src[:, h])
+            k = slice(0, 2 * P) if nh is None else slice(P * nh, P * (nh + 1))
+            dst = rb[r][:].rearrange("b (u q e) -> b u q e", u=2, e=2)[:, :, k]
+            src = res[r][:, c].rearrange("b (q u e) -> b u q e", u=2, e=2)
+            if eng == "s":
+                nc.scalar.copy(out=dst, in_=src)
+            elif eng == "g":
+                nc.gpsimd.tensor_scalar(out=dst, in0=src, scalar1=1.0, scalar2=0.0, op0=ALU.mult, op1=ALU.add)
+            else:
+                nc.vector.tensor_copy(out=dst, in_=src)
 
         def r_transpose(r, nh=None):
             if r not in rt:
@@ -291,7 +287,7 @@ def tile_escmdoublyrobusterrormap_x2_kernel(tc, x, w_words, w_scales, g, wh, o, 
             words = rb[r][:].bitcast(F32)
             for gg in range(2) if nh is None else (nh,):
                 for uu in range(2):
-                    k = 256 * gg + P * uu
+                    k = 256 * uu + P * gg
                     nc.tensor.transpose(rt[r][:, gg, uu, :], words[:, k : k + P], ident[:])
 
         def r_copy(r, eng="s", nh=None):
@@ -343,211 +339,212 @@ def tile_escmdoublyrobusterrormap_x2_kernel(tc, x, w_words, w_scales, g, wh, o, 
             return 0 <= r < ROWS
 
         with tc.manual_schedule():
-            x_transpose(0)
             wh_interleave(*units[0], "v")
+            x_transpose(0)
             x_copy(0, "v")
+            x_transpose(1)
             wh_quant(*units[0])
             x_quant(0)
             trunk(0)
-            x_transpose(1)
-            wh_interleave(*units[1], "v")
             x_copy(1, "s")
-            wh_interleave(*units[2], "v")
+            wh_interleave(*units[1], "v")
             tanh(0)
-            wh_quant(*units[1])
+            wh_interleave(*units[2], "v")
+            x_quant(1)
+            wh_interleave(*units[3], "s")
             h_transpose(0)
             h_gain(0)
-            wh_interleave(*units[3], "s")
-            x_quant(1)
+            wh_quant(*units[1])
             h_quant(0)
-            wh_interleave(*units[5], "v")
+            wh_quant(*units[2])
             trunk(1)
             head(0, 0, 1)
-            wh_quant(*units[3])
-            wh_quant(*units[5])
             tanh(1)
-            x_transpose(2)
             tanh1(0, 0)
+            x_transpose(2)
             h_transpose(1)
-            head(0, 1, 1)
+            wh_interleave(*units[4], "v")
+            wh_quant(*units[3])
             subtract(0, 0)
             x_transpose(3)
-            x_copy(2, "s")
             h_gain(1)
-            x_quant(2)
-            trunk(2)
+            x_copy(2, "s")
             square(0, 0)
-            wh_interleave(*units[4], "v")
-            h_quant(1)
+            head(0, 1, 1)
+            x_quant(2)
+            head(0, 1, 0)
             tanh1(0, 1)
-            wh_quant(*units[2])
-            head(0, 1, 2)
-            wh_quant(*units[4])
+            trunk(2)
             head(0, 0, 0)
-            tanh(2)
+            wh_interleave(*units[5], "v")
+            x_copy(3, "s")
+            h_quant(1)
+            exp0(0, 1)
+            wh_quant(*units[4])
             exp0(0, 0)
             subtract(0, 1)
-            inv_half(0, 0)
-            h_transpose(2)
-            weight_half(0, 0, "g")
-            x_copy(3, "s")
-            square(0, 1)
-            head(0, 1, 0)
-            head(1, 0, 1)
-            x_transpose(5)
-            x_transpose(4)
-            exp0(0, 1)
+            tanh(2)
             x_quant(3)
-            h_gain(2)
-            tanh1(1, 0)
-            diff(0, 1)
-            head(1, 1, 0)
-            exp0(1, 1)
-            head(0, 0, 2)
-            inv_half(0, 1)
-            h_quant(2)
-            x_copy(5, "v")
-            trunk(3)
-            diff(0, 0)
-            x_copy(4, "s")
-            weight_half(0, 1, "g")
+            x_transpose(4)
+            wh_quant(*units[5])
+            head(1, 0, 0)
             head(1, 1, 1)
+            head(0, 0, 2)
+            inv_half(0, 0)
+            x_transpose(5)
+            exp0(1, 0)
+            square(0, 1)
+            h_transpose(2)
+            head(1, 0, 1)
+            inv_half(0, 1)
+            weight_half(0, 0, "v")
+            x_copy(4, "s")
+            diff(0, 0)
+            tanh1(1, 0)
+            h_gain(2)
+            head(0, 1, 2)
+            diff(0, 1)
+            weight_half(0, 1, "g")
+            tanh1(1, 1)
+            trunk(3)
+            head(1, 1, 0)
+            subtract(1, 0)
+            tanh(3)
+            h_quant(2)
+            exp0(1, 1)
+            square(1, 0)
+            inv_half(1, 0)
             x_quant(4)
             prod(0)
-            tanh1(1, 1)
-            subtract(1, 0)
+            x_copy(5, "s")
+            h_transpose(3)
+            head(2, 0, 0)
+            inv_half(1, 1)
+            weight_half(1, 0, "v")
             for s in range(1, 6):
-                if ok(s + 5):
-                    x_transpose(s + 5)
-                if ok(s - 2):
-                    round_r(s - 2, "v", 0)
-                square(s, 0)
+                exp0(s + 1, 0)
                 head(s + 1, 0, 1)
-                head(s, 0, 0)
-                inv_half(s, 1)
-                if (s - 4) % 2 == 1 and s - 4 > 0:
-                    r_quant((s - 4) // 2)
-                tanh(s + 2)
-                subtract(s, 1)
-                if ok(s + 4):
-                    x_quant(s + 4)
-                tanh1(s + 1, 0)
-                weight_half(s, 1, "g")
-                result(s - 1, 1)
-                if ok(s - 3):
-                    r_transpose(s - 3)
-                exp0(s, 0)
-                result(s - 1, 0)
-                h_transpose(s + 2)
-                inv_half(s, 0)
-                head(s + 1, 1, 1)
-                head(s + 1, 1, 0)
                 if ok(s - 2):
-                    round_r(s - 2, "s", 1)
-                head(s, 0, 2)
-                square(s, 1)
-                h_gain(s + 2)
-                if (s - 4) % 2 == 1 and s - 4 > 0:
-                    store_scales((s - 4) // 2)
-                head(s, 1, 2)
-                if ok(s + 5):
-                    x_copy(s + 5, "s")
-                diff(s, 0)
-                if (s - 4) % 2 == 1 and s - 4 > 0:
-                    store_words((s - 4) // 2)
-                diff(s, 1)
-                h_quant(s + 2)
-                exp0(s + 1, 1)
-                weight_half(s, 0, "g")
-                subtract(s + 1, 0)
+                    store_r(s - 2, 0)
                 if ok(s - 2):
                     store_r(s - 2, 1)
-                prod(s)
-                if ok(s - 3):
-                    r_copy(s - 3, "s")
-                tanh1(s + 1, 1)
+                subtract(s, 1)
+                result(s - 1, 0)
+                if ok(s + 5):
+                    x_transpose(s + 5)
+                tanh1(s + 1, 0)
+                h_gain(s + 2)
+                result(s - 1, 1)
+                if ok(s + 4):
+                    x_quant(s + 4)
+                square(s, 1)
+                head(s + 1, 1, 0)
+                head(s, 0, 2)
+                head(s + 1, 1, 1)
+                head(s, 1, 2)
+                weight_half(s, 1, "g")
+                diff(s, 0)
+                if ok(s - 2):
+                    round_r(s - 2, "s")
+                if ok(s - 4):
+                    r_copy(s - 4, "s")
+                h_quant(s + 2)
+                diff(s, 1)
                 if ok(s + 3):
                     trunk(s + 3)
-                store_r(s - 1, 0)
-            square(6, 0)
-            head(6, 0, 0)
-            store_r(4, 1)
-            exp0(6, 0)
+                if ok(s + 5):
+                    x_copy(s + 5, "s")
+                subtract(s + 1, 0)
+                tanh1(s + 1, 1)
+                inv_half(s + 1, 0)
+                prod(s)
+                exp0(s + 1, 1)
+                if ok(s - 2):
+                    r_transpose(s - 2)
+                head(s + 2, 0, 0)
+                if ok(s + 3):
+                    tanh(s + 3)
+                weight_half(s + 1, 0, "v")
+                if (s - 4) % 2 == 1 and s - 4 > 0:
+                    r_quant((s - 4) // 2)
+                inv_half(s + 1, 1)
+                square(s + 1, 0)
+                if (s - 4) % 2 == 1 and s - 4 > 0:
+                    store_scales((s - 4) // 2)
+                if (s - 4) % 2 == 1 and s - 4 > 0:
+                    store_words((s - 4) // 2)
+                if ok(s + 3):
+                    h_transpose(s + 3)
             subtract(6, 1)
-            inv_half(6, 0)
-            head(7, 0, 1)
-            r_transpose(3)
-            inv_half(6, 1)
-            result(5, 0)
-            round_r(4, "s", 0)
-            round_r(4, "s", 1)
-            head(6, 0, 2)
-            square(6, 1)
-            tanh1(7, 0)
-            result(5, 1)
-            head(7, 0, 0)
             r_copy(3, "s")
-            head(6, 1, 2)
-            diff(6, 0)
-            subtract(7, 0)
-            diff(6, 1)
-            r_quant(1)
-            store_scales(1)
-            weight_half(6, 0, "g")
+            store_r(4, 1)
             exp0(7, 0)
+            result(5, 0)
+            square(6, 1)
+            store_r(4, 0)
+            head(7, 0, 1)
             head(7, 1, 0)
-            square(7, 0)
-            head(7, 1, 1)
-            round_r(5, "s", 0)
-            tanh1(7, 1)
-            subtract(7, 1)
-            weight_half(6, 1, "g")
-            prod(6)
+            head(6, 0, 2)
+            result(5, 1)
+            head(6, 1, 2)
             exp0(7, 1)
+            tanh1(7, 0)
+            diff(6, 0)
+            r_copy(2, "s")
             inv_half(7, 0)
-            store_r(5, 1)
+            weight_half(6, 1, "g")
+            diff(6, 1)
+            weight_half(7, 0, "v")
+            prod(6)
+            subtract(7, 0)
+            r_quant(1)
+            head(7, 1, 1)
+            round_r(4, "s")
+            square(7, 0)
             result(6, 0)
-            round_r(5, "s", 1)
+            tanh1(7, 1)
             r_transpose(4)
-            head(7, 0, 2)
-            result(6, 1)
-            weight_half(7, 0, "g")
+            subtract(7, 1)
             inv_half(7, 1)
-            square(7, 1)
-            head(7, 1, 2)
-            round_r(6, "s", 1)
-            store_words(1)
-            diff(7, 0)
-            round_r(6, "s", 0)
-            diff(7, 1)
+            result(6, 1)
             r_copy(4, "s")
-            weight_half(7, 1, "g")
-            prod(7, 1)
-            r_transpose(5)
-            r_transpose(6)
+            square(7, 1)
+            round_r(5, "s")
             store_r(5, 0)
-            r_copy(5, "s")
-            prod(7, 0)
-            r_copy(6, "s")
-            result(7, 1)
-            store_r(6, 1)
-            result(7, 0)
-            r_quant(2)
-            round_r(7, "s", 1)
             store_r(6, 0)
-            r_quant(3, 0, 1)
-            store_r(7, 1)
-            store_r(7, 0)
+            round_r(6, "s")
+            head(7, 0, 2)
+            head(7, 1, 2)
+            diff(7, 0)
+            diff(7, 1)
+            r_transpose(5)
+            r_copy(5, "s")
+            weight_half(7, 1, "g")
+            r_transpose(6)
+            prod(7, 0)
+            prod(7, 1)
+            store_scales(1)
+            store_r(6, 1)
+            r_copy(6, "s")
+            result(7, 0)
+            result(7, 1)
+            r_quant(2)
             round_r(7, "s", 0)
-            r_transpose(7, 1)
-            r_quant(3, 0, 0)
-            r_copy(7, "s", 1)
-            store_words(2)
+            round_r(7, "s", 1)
             r_transpose(7, 0)
+            store_words(1)
+            r_transpose(7, 1)
+            r_copy(7, "v", 0)
+            store_r(5, 1)
+            r_quant(3, 0, 0)
+            r_quant(3, 0, 1)
+            r_copy(7, "s", 1)
+            r_quant(3, 1, 0)
+            store_r(7, 0)
+            store_r(7, 1)
+            store_words(2)
+            r_quant(3, 1, 1)
             store_words(3, 0)
             store_scales(2)
-            r_copy(7, "v", 0)
-            r_quant(3, 1, 1)
-            r_quant(3, 1, 0)
             store_words(3, 1)
             store_scales(3)

@@ -14,537 +14,574 @@ ACT = mybir.ActivationFunctionType
 ALU = mybir.AluOpType
 
 P = 128
-B, D, H, N, T = 1024, 1024, 512, 1024, 3
-ROWS = B // P
+PACK = 4
+B, D, H, N, HEADS = 1024, 1024, 512, 1024, 3
+GROUP = P * PACK
+X_GROUPS = D // GROUP
 HALF = 512
-FLOPS = 2 * B * D * H + T * 2 * B * H * N
+HALVES = N // HALF
+ROWS = B // P
+P_FLOOR = 0.2
+FLOPS = 2 * B * D * H + HEADS * 2 * B * H * N
 
 
 def tile_escmdoublyrobusterrormap_x2_kernel(tc, x, w_words, w_scales, g, wh, o, y, out_0, out_1, out_2):
     nc = tc.nc
+    on_vector, on_scalar = nc.vector.tensor_copy, nc.scalar.copy
+
     with ExitStack() as ctx:
         const = ctx.enter_context(tc.tile_pool(name="const", bufs=1))
-        ld = ctx.enter_context(tc.tile_pool(name="ld", bufs=8))
-        wraw = ctx.enter_context(tc.tile_pool(name="wraw", bufs=6))
-        st = ctx.enter_context(tc.tile_pool(name="st", bufs=2))
-        st3 = ctx.enter_context(tc.tile_pool(name="st3", bufs=3))
-        ps_1 = ctx.enter_context(tc.psum_pool(name="ps1", bufs=1))
-        ps_2 = ctx.enter_context(tc.psum_pool(name="ps2", bufs=2))
+        blocks = ctx.enter_context(tc.tile_pool(name="blocks", bufs=ROWS))
+        raw_heads = ctx.enter_context(tc.tile_pool(name="raw_heads", bufs=2))
+        head_pairs = ctx.enter_context(tc.tile_pool(name="head_pairs", bufs=HEADS * HALVES))
+        two = ctx.enter_context(tc.tile_pool(name="two", bufs=2))
+        three = ctx.enter_context(tc.tile_pool(name="three", bufs=3))
+        bank = ctx.enter_context(tc.psum_pool(name="bank", bufs=1))
+        banks = ctx.enter_context(tc.psum_pool(name="banks", bufs=2))
 
         ident = const.tile([P, P], F32, name="ident", align_bytes=64)
-        minus2 = const.tile([P, P], BF16, name="minus2", align_bytes=64)
-        warm = const.tile([P, 1], F32, name="warm")
-        w_codes = const.tile([P, 2, 2 * H], U8, name="w_codes", align_bytes=64)
-        w_plane = const.tile([P, 2, H], U8, name="w_plane", align_bytes=64)
-        gain = const.tile([P, 4], BF16, name="gain", align_bytes=64)
+        minus_two = const.tile([P, P], BF16, name="minus_two", align_bytes=64)
+        first = const.tile([P, 1], F32, name="first")
+        w_codes = const.tile([P, X_GROUPS, 2 * H], U8, name="w_codes", align_bytes=64)
+        w_plane = const.tile([P, X_GROUPS, H], U8, name="w_plane", align_bytes=64)
+        gain = const.tile([P, PACK], BF16, name="gain", align_bytes=64)
 
         nc.vector.memset(w_plane[:].rearrange("p g n -> p (g n)").bitcast(I32), 0)
-        nc.vector.memset(warm[:], 0.0)
+        nc.vector.memset(first[:], 0.0)
         make_identity(nc, ident[:])
-        nc.scalar.activation(out=warm[:], in_=warm[:], func=ACT.Exp)
-        nc.vector.tensor_scalar(out=minus2[:], in0=ident[:], scalar1=-2.0, scalar2=None, op0=ALU.mult)
+        nc.scalar.activation(out=first[:], in_=first[:], func=ACT.Exp)
+        nc.vector.tensor_scalar(out=minus_two[:], in0=ident[:], scalar1=-2.0, scalar2=None, op0=ALU.mult)
+
+        def half(c):
+            return slice(HALF * c, HALF * (c + 1))
+
+        def chunk(i):
+            return slice(P * i, P * (i + 1))
 
         x_sb, o_sb, y_sb, wh_raw = {}, {}, {}, {}
 
         def load_x(r):
-            x_sb[r] = ld.tile([P, D], BF16, name="x_sb", align_bytes=64)
-            nc.sync.dma_start(out=x_sb[r][:], in_=x[P * r : P * (r + 1), :])
+            x_sb[r] = blocks.tile([P, D], BF16, name="x_sb", align_bytes=64)
+            nc.sync.dma_start(out=x_sb[r][:], in_=x[chunk(r), :])
 
         def load_oy(r):
-            o_sb[r] = ld.tile([P, N], BF16, name="o_sb", align_bytes=64)
-            nc.sync.dma_start(out=o_sb[r][:], in_=o[P * r : P * (r + 1), :])
-            y_sb[r] = ld.tile([P, N], BF16, name="y_sb", align_bytes=64)
-            nc.sync.dma_start(out=y_sb[r][:], in_=y[P * r : P * (r + 1), :])
+            o_sb[r] = blocks.tile([P, N], BF16, name="o_sb", align_bytes=64)
+            nc.sync.dma_start(out=o_sb[r][:], in_=o[chunk(r), :])
+            y_sb[r] = blocks.tile([P, N], BF16, name="y_sb", align_bytes=64)
+            nc.sync.dma_start(out=y_sb[r][:], in_=y[chunk(r), :])
 
-        def load_wh(t, nh):
-            wh_raw[t, nh] = wraw.tile([P, 4, HALF], BF16, name="wh_raw", align_bytes=64)
+        def load_head_half(t, c):
+            raw = raw_heads.tile([P, PACK, HALF], BF16, name="raw_half", align_bytes=64)
+            nc.sync.dma_start(out=raw[:], in_=wh[t].rearrange("(p j) n -> p j n", j=PACK)[:, :, half(c)])
+            wh_raw[t, c] = raw[:]
+
+        def load_head(t):
+            raw = raw_heads.tile([P, PACK, N], BF16, name="raw_head", align_bytes=64)
+            nc.sync.dma_start(out=raw[:], in_=wh[t].rearrange("(p j) n -> p j n", j=PACK))
+            for c in range(HALVES):
+                wh_raw[t, c] = raw[:, :, half(c)]
+
+        def load_w_scales():
+            for q in range(4):
+                rows = w_plane[32 * q : 32 * q + 4].rearrange("p g n -> p (g n)").bitcast(I32)
+                nc.sync.dma_start(
+                    out=rows.rearrange("p (g n) -> p g n", g=X_GROUPS),
+                    in_=w_scales.bitcast(I32)[:, 4 * q : 4 * q + 4, :].rearrange("g r n -> r g n"),
+                )
+
+        def load_w_codes():
+            words = w_codes[:].rearrange("p g n -> p (g n)").bitcast(I32)
             nc.sync.dma_start(
-                out=wh_raw[t, nh][:],
-                in_=wh[t].rearrange("(p j) n -> p j n", j=4)[:, :, HALF * nh : HALF * (nh + 1)],
+                out=words.rearrange("p (g n) -> p g n", g=X_GROUPS),
+                in_=w_words.bitcast(I32).rearrange("g p n -> p g n"),
             )
 
-        units = [(0, 0), (1, 0), (0, 1), (1, 1), (2, 0), (2, 1)]
-        load_wh(*units[0])
+        def load_gain():
+            nc.sync.dma_start(out=gain[:], in_=g.rearrange("(p t) -> p t", t=PACK))
+
+        load_head_half(0, 0)
         load_x(0)
-        nc.sync.dma_start(
-            out=w_codes[:].rearrange("p g n -> p (g n)").bitcast(I32).rearrange("p (g n) -> p g n", g=2),
-            in_=w_words.bitcast(I32).rearrange("g p n -> p g n"),
-        )
-        for q in range(4):
-            nc.sync.dma_start(
-                out=w_plane[32 * q : 32 * q + 4].rearrange("p g n -> p (g n)").bitcast(I32).rearrange("p (g n) -> p g n", g=2),
-                in_=w_scales.bitcast(I32)[:, 4 * q : 4 * q + 4, :].rearrange("g r n -> r g n"),
-            )
-        nc.sync.dma_start(out=gain[:], in_=g.rearrange("(p t) -> p t", t=4))
-        load_wh(*units[1])
+        load_w_scales()
+        load_w_codes()
+        load_head(1)
         load_x(1)
-        load_wh(*units[2])
-        load_wh(*units[3])
-        load_wh(*units[4])
-        load_wh(*units[5])
+        load_gain()
+        load_head_half(0, 1)
+        load_head(2)
         load_x(2)
         load_oy(0)
         load_x(3)
-        load_oy(1)
-        for r in range(2, ROWS):
-            if r + 2 < ROWS:
-                load_x(r + 2)
+        for r in range(1, ROWS):
             load_oy(r)
+            if r + 3 < ROWS:
+                load_x(r + 3)
 
-        wh_il, wh_codes, wh_scales = {}, {}, {}
-        xt, xg, xq, xs, u_ps, th, ht, hb, hq, hs = ({} for _ in range(10))
-        z, a0, t1, err, d, res, rb, rt, pg = ({} for _ in range(9))
-        pq, psc, qb = {}, {}, {}
+        wh_words, wh_codes, wh_scales = {}, {}, {}
 
-        def wh_interleave(t, nh, eng):
-            wh_il[t, nh] = wraw.tile([P, HALF, 4], BF16, name="wh_il", align_bytes=64)
-            src = wh_raw[t, nh][:].rearrange("p j (c i) -> p c j i", i=4)
-            dst = wh_il[t, nh][:].rearrange("p (c i) j -> p c j i", i=4)
-            if eng == "v":
-                nc.vector.tensor_copy(out=dst, in_=src)
-            elif eng == "s":
-                nc.scalar.copy(out=dst, in_=src)
-            else:
-                nc.gpsimd.tensor_scalar(out=dst, in0=src, scalar1=1.0, scalar2=0.0, op0=ALU.mult, op1=ALU.add)
-
-        def wh_quant(t, nh):
-            wh_codes[t, nh] = const.tile([P, HALF], U32, name="whc%d%d" % (t, nh), align_bytes=64)
-            wh_scales[t, nh] = const.tile([P, HALF], U8, name="whs%d%d" % (t, nh), align_bytes=64)
-            nc.vector.quantize_mx(
-                out=wh_codes[t, nh][:].bitcast(FP8X4),
-                scales=wh_scales[t, nh][:],
-                in_=wh_il[t, nh][:].rearrange("p n j -> p (n j)"),
+        def head_interleave(t, c, copy):
+            wh_words[t, c] = head_pairs.tile([P, HALF, PACK], BF16, name="wh_words", align_bytes=64)
+            copy(
+                out=wh_words[t, c][:].rearrange("p (n i) j -> p n j i", i=4),
+                in_=wh_raw[t, c].rearrange("p j (n i) -> p n j i", i=4),
             )
 
-        def x_transpose(r):
-            xt[r] = ps_2.tile([P, 2, 2, P], F32, name="xt", tag="turn")
-            words = x_sb[r][:].bitcast(F32)
-            for gg in range(2):
-                for uu in range(2):
-                    nc.tensor.transpose(xt[r][:, gg, uu, :], words[:, 256 * gg + uu : 256 * (gg + 1) : 2], ident[:])
-
-        def x_copy(r, eng):
-            xg[r] = st.tile([P, 2, P, 4], BF16, name="xg", align_bytes=64)
-            dst = xg[r][:].rearrange("p g b t -> p (g b t)").bitcast(F32).rearrange("p (g b u) -> p g b u", g=2, u=2)
-            src = xt[r][:].rearrange("p g u b -> p g b u")
-            if eng == "s":
-                nc.scalar.copy(out=dst, in_=src)
-            else:
-                nc.vector.tensor_copy(out=dst, in_=src)
-
-        def x_quant(r):
-            xq[r] = st.tile([P, 2 * P], U32, name="xq", align_bytes=64)
-            xs[r] = st.tile([P, 2 * P], U8, name="xs", align_bytes=64)
+        def head_quantise(t, c):
+            wh_codes[t, c] = const.tile([P, HALF], U32, name="wh_codes_%d_%d" % (t, c), align_bytes=64)
+            wh_scales[t, c] = const.tile([P, HALF], U8, name="wh_scales_%d_%d" % (t, c), align_bytes=64)
             nc.vector.quantize_mx(
-                out=xq[r][:].bitcast(FP8X4), scales=xs[r][:], in_=xg[r][:].rearrange("p g b t -> p (g b t)")
+                out=wh_codes[t, c][:].bitcast(FP8X4),
+                scales=wh_scales[t, c][:],
+                in_=wh_words[t, c][:].rearrange("p n j -> p (n j)"),
+            )
+
+        x_turned, x_words, x_codes, x_scales = {}, {}, {}, {}
+        trunk_sum, trunk_tanh, trunk_turned, h_words, h_codes, h_scales = {}, {}, {}, {}, {}, {}
+
+        def by_word(tile):
+            words = tile[:].rearrange("p g b t -> p (g b t)").bitcast(F32)
+            return words.rearrange("p (g b u) -> p g b u", g=2, u=2)
+
+        def x_transpose(r):
+            x_turned[r] = banks.tile([P, X_GROUPS, 2, P], F32, name="x_turned", tag="turned")
+            words = x_sb[r][:].bitcast(F32)
+            for gg in range(X_GROUPS):
+                for u in range(2):
+                    pairs = words[:, 256 * gg + u : 256 * (gg + 1) : 2]
+                    nc.tensor.transpose(x_turned[r][:, gg, u, :], pairs, ident[:])
+
+        def x_interleave(r, copy):
+            x_words[r] = two.tile([P, X_GROUPS, P, PACK], BF16, name="x_words", align_bytes=64)
+            copy(out=by_word(x_words[r]), in_=x_turned[r][:].rearrange("p g u b -> p g b u"))
+
+        def x_quantise(r):
+            x_codes[r] = two.tile([P, X_GROUPS * P], U32, name="x_codes", align_bytes=64)
+            x_scales[r] = two.tile([P, X_GROUPS * P], U8, name="x_scales", align_bytes=64)
+            nc.vector.quantize_mx(
+                out=x_codes[r][:].bitcast(FP8X4),
+                scales=x_scales[r][:],
+                in_=x_words[r][:].rearrange("p g b t -> p (g b t)"),
             )
 
         def trunk(r):
-            u_ps[r] = ps_1.tile([P, H], F32, name="u", tag="trunk")
-            for gg in range(2):
+            trunk_sum[r] = bank.tile([P, H], F32, name="trunk_sum", tag="trunk")
+            for gg in range(X_GROUPS):
                 nc.tensor.matmul_mx(
-                    out=u_ps[r][:],
-                    lhsT=xq[r][:, P * gg : P * (gg + 1)].bitcast(FP8X4),
-                    lhsT_scale=xs[r][:, P * gg : P * (gg + 1)],
+                    out=trunk_sum[r][:],
+                    lhsT=x_codes[r][:, chunk(gg)].bitcast(FP8X4),
+                    lhsT_scale=x_scales[r][:, chunk(gg)],
                     rhs=w_codes[:, gg, :].bitcast(FP4X4),
                     rhs_scale=w_plane[:, gg, :],
                     start=(gg == 0),
-                    stop=(gg == 1),
+                    stop=(gg == X_GROUPS - 1),
                 )
 
-        def tanh(r):
-            th[r] = st.tile([P, 4, P], F32, name="th", align_bytes=64)
-            nc.scalar.activation(out=th[r][:], in_=u_ps[r][:].rearrange("b (p t) -> b t p", t=4), func=ACT.Tanh)
+        def tanh_trunk(r):
+            trunk_tanh[r] = two.tile([P, PACK, P], F32, name="trunk_tanh", align_bytes=64)
+            nc.scalar.activation(
+                out=trunk_tanh[r][:], in_=trunk_sum[r][:].rearrange("b (p t) -> b t p", t=PACK), func=ACT.Tanh
+            )
 
         def h_transpose(r):
-            ht[r] = ps_1.tile([P, 4, P], F32, name="ht", tag="trunk")
-            for t in range(4):
-                nc.tensor.transpose(ht[r][:, t, :], th[r][:, t, :], ident[:])
+            trunk_turned[r] = bank.tile([P, PACK, P], F32, name="trunk_turned", tag="trunk")
+            for t in range(PACK):
+                nc.tensor.transpose(trunk_turned[r][:, t, :], trunk_tanh[r][:, t, :], ident[:])
 
         def h_gain(r):
-            hb[r] = st.tile([P, P, 4], BF16, name="hb", align_bytes=64)
+            h_words[r] = two.tile([P, P, PACK], BF16, name="h_words", align_bytes=64)
             nc.vector.tensor_tensor(
-                out=hb[r][:],
-                in0=ht[r][:].rearrange("p t b -> p b t"),
-                in1=gain[:].unsqueeze(1).to_broadcast([P, P, 4]),
+                out=h_words[r][:],
+                in0=trunk_turned[r][:].rearrange("p t b -> p b t"),
+                in1=gain[:].unsqueeze(1).to_broadcast([P, P, PACK]),
                 op=ALU.mult,
             )
 
-        def h_quant(r):
-            hq[r] = st3.tile([P, P], U32, name="hq", align_bytes=64)
-            hs[r] = st3.tile([P, P], U8, name="hs", align_bytes=64)
+        def h_quantise(r):
+            h_codes[r] = three.tile([P, P], U32, name="h_codes", align_bytes=64)
+            h_scales[r] = three.tile([P, P], U8, name="h_scales", align_bytes=64)
             nc.vector.quantize_mx(
-                out=hq[r][:].bitcast(FP8X4), scales=hs[r][:], in_=hb[r][:].rearrange("p b t -> p (b t)")
+                out=h_codes[r][:].bitcast(FP8X4),
+                scales=h_scales[r][:],
+                in_=h_words[r][:].rearrange("p b t -> p (b t)"),
             )
 
-        def head(r, nh, t):
-            if t < 2:
-                z[r, nh, t] = ps_2.tile([P, HALF], F32, name="z01")
-            else:
-                z[r, nh, t] = ps_2.tile([P, HALF], F32, name="z2")
-            if t == 1:
-                for c in range(4):
-                    k = slice(P * c, P * (c + 1))
-                    nc.tensor.matmul_mx(
-                        out=z[r, nh, t][:, k],
-                        lhsT=wh_codes[t, nh][:, k].bitcast(FP8X4),
-                        lhsT_scale=wh_scales[t, nh][:, k],
-                        rhs=hq[r][:].bitcast(FP8X4),
-                        rhs_scale=hs[r][:],
-                        start=True,
-                        stop=True,
-                    )
-                return
+        z, difference = {}, {}
+        weight, z1_tanh, err, delta, result = {}, {}, {}, {}, {}
+
+        def row_tile(store, r, name, dtype=F32):
+            if r not in store:
+                store[r] = three.tile([P, N], dtype, name=name, align_bytes=64)
+            return store[r]
+
+        def head_0(r, c):
+            head_product(r, c, 0, "z01")
+
+        def head_2(r, c):
+            head_product(r, c, 2, "z2")
+
+        def head_product(r, c, t, tag):
+            z[r, c, t] = banks.tile([P, HALF], F32, name="z_%d" % t, tag=tag)
             nc.tensor.matmul_mx(
-                out=z[r, nh, t][:],
-                lhsT=hq[r][:].bitcast(FP8X4),
-                lhsT_scale=hs[r][:],
-                rhs=wh_codes[t, nh][:].bitcast(FP8X4),
-                rhs_scale=wh_scales[t, nh][:],
+                out=z[r, c, t][:],
+                lhsT=h_codes[r][:].bitcast(FP8X4),
+                lhsT_scale=h_scales[r][:],
+                rhs=wh_codes[t, c][:].bitcast(FP8X4),
+                rhs_scale=wh_scales[t, c][:],
                 start=True,
                 stop=True,
             )
 
-        def cols(nh):
-            return slice(HALF * nh, HALF * (nh + 1))
+        def head_1(r, c):
+            z[r, c, 1] = banks.tile([P, HALF], F32, name="z_1", tag="z01")
+            for i in range(HALF // P):
+                nc.tensor.matmul_mx(
+                    out=z[r, c, 1][:, chunk(i)],
+                    lhsT=wh_codes[1, c][:, chunk(i)].bitcast(FP8X4),
+                    lhsT_scale=wh_scales[1, c][:, chunk(i)],
+                    rhs=h_codes[r][:].bitcast(FP8X4),
+                    rhs_scale=h_scales[r][:],
+                    start=True,
+                    stop=True,
+                )
 
-        def get(store, r, name, dt=F32):
-            if r not in store:
-                store[r] = st3.tile([P, N], dt, name=name, align_bytes=64)
-            return store[r]
+        def exp_0(r, c):
+            tile = row_tile(weight, r, "weight")
+            nc.scalar.activation(out=tile[:, half(c)], in_=z[r, c, 0][:], func=ACT.Exp, scale=-1.0)
 
-        def exp0(r, nh):
-            nc.scalar.activation(out=get(a0, r, "a0")[:, cols(nh)], in_=z[r, nh, 0][:], func=ACT.Exp, scale=-1.0)
+        def tanh_1(r, c):
+            tile = row_tile(z1_tanh, r, "z1_tanh")
+            nc.scalar.activation(out=tile[:, half(c)], in_=z[r, c, 1][:], func=ACT.Tanh, scale=0.5)
 
-        def tanh1(r, nh):
-            nc.scalar.activation(out=get(t1, r, "t1")[:, cols(nh)], in_=z[r, nh, 1][:], func=ACT.Tanh, scale=0.5)
-
-        def subtract(r, nh):
-            q = qb[r, nh] = ps_1.tile([P, HALF], F32, name="qb")
-            nc.tensor.matmul(q[:], lhsT=minus2[:], rhs=y_sb[r][:, cols(nh)], start=True, stop=False)
-            for c in range(4):
-                k = slice(P * c, P * (c + 1))
+        def subtract(r, c):
+            difference[r, c] = bank.tile([P, HALF], F32, name="difference")
+            nc.tensor.matmul(
+                difference[r, c][:], lhsT=minus_two[:], rhs=y_sb[r][:, half(c)], start=True, stop=False
+            )
+            last = HALF // P - 1
+            for i in range(HALF // P):
                 nc.tensor.matmul(
-                    q[:, k], lhsT=t1[r][:, HALF * nh + P * c : HALF * nh + P * (c + 1)], rhs=ident[:],
-                    is_transpose=True, start=False, stop=(c == 3),
+                    difference[r, c][:, chunk(i)],
+                    lhsT=z1_tanh[r][:, chunk(HALF // P * c + i)],
+                    rhs=ident[:],
+                    is_transpose=True,
+                    start=False,
+                    stop=(i == last),
                 )
 
-        def square(r, nh):
-            nc.scalar.activation(out=get(err, r, "err")[:, cols(nh)], in_=qb[r, nh][:], func=ACT.Square, scale=0.5, bias=0.5)
+        def square(r, c):
+            tile = row_tile(err, r, "err")
+            nc.scalar.activation(
+                out=tile[:, half(c)], in_=difference[r, c][:], func=ACT.Square, scale=0.5, bias=0.5
+            )
 
-        def inv_p(r):
-            nc.vector.tensor_scalar(out=a0[r][:], in0=a0[r][:], scalar1=1.0, scalar2=5.0, op0=ALU.add, op1=ALU.min)
-
-        def inv_half(r, nh):
-            c = cols(nh)
+        def inverse_p(r, c):
             nc.vector.tensor_scalar(
-                out=a0[r][:, c], in0=a0[r][:, c], scalar1=1.0, scalar2=5.0, op0=ALU.add, op1=ALU.min
+                out=weight[r][:, half(c)],
+                in0=weight[r][:, half(c)],
+                scalar1=1.0,
+                scalar2=1.0 / P_FLOOR,
+                op0=ALU.add,
+                op1=ALU.min,
             )
 
-        def weight(r, eng="v"):
-            e = nc.gpsimd if eng == "g" else nc.vector
-            e.tensor_tensor(out=a0[r][:], in0=a0[r][:], in1=o_sb[r][:], op=ALU.mult)
+        def times_o(r, c):
+            nc.gpsimd.tensor_tensor(
+                out=weight[r][:, half(c)], in0=weight[r][:, half(c)], in1=o_sb[r][:, half(c)], op=ALU.mult
+            )
 
-        def weight_half(r, nh, eng):
-            c = cols(nh)
-            e = nc.gpsimd if eng == "g" else nc.vector
-            e.tensor_tensor(out=a0[r][:, c], in0=a0[r][:, c], in1=o_sb[r][:, c], op=ALU.mult)
+        def err_less_e(r, c):
+            tile = row_tile(delta, r, "delta")
+            nc.vector.tensor_tensor(
+                out=tile[:, half(c)], in0=err[r][:, half(c)], in1=z[r, c, 2][:], op=ALU.subtract
+            )
 
-        def diff(r, nh):
-            c = cols(nh)
-            get(d, r, "d")
-            nc.vector.tensor_tensor(out=d[r][:, c], in0=err[r][:, c], in1=z[r, nh, 2][:], op=ALU.subtract)
+        def weighted(r, columns=slice(0, N)):
+            nc.vector.tensor_tensor(
+                out=delta[r][:, columns], in0=weight[r][:, columns], in1=delta[r][:, columns], op=ALU.mult
+            )
 
-        def prod(r, nh=None):
-            c = slice(0, N) if nh is None else cols(nh)
-            nc.vector.tensor_tensor(out=d[r][:, c], in0=a0[r][:, c], in1=d[r][:, c], op=ALU.mult)
+        def add_e(r, c):
+            tile = row_tile(result, r, "result")
+            nc.vector.tensor_tensor(
+                out=tile[:, half(c)], in0=z[r, c, 2][:], in1=delta[r][:, half(c)], op=ALU.add
+            )
 
-        def result(r, nh):
-            c = cols(nh)
-            get(res, r, "res")
-            nc.vector.tensor_tensor(out=res[r][:, c], in0=z[r, nh, 2][:], in1=d[r][:, c], op=ALU.add)
+        def store_result(r, c):
+            nc.sync.dma_start(out=out_0[chunk(r), half(c)], in_=result[r][:, half(c)])
 
-        def store_r(r, nh):
-            c = cols(nh)
-            nc.sync.dma_start(out=out_0[P * r : P * (r + 1), c], in_=res[r][:, c])
+        rounded, turned, plane_words, plane_codes, plane_scales = {}, {}, {}, {}, {}
 
-        def round_r(r, eng, nh=None):
-            get(rb, r, "rb", BF16)
-            c = slice(0, N) if nh is None else cols(nh)
-            k = slice(0, 2 * P) if nh is None else slice(P * nh, P * (nh + 1))
-            dst = rb[r][:].rearrange("b (u q e) -> b u q e", u=2, e=2)[:, :, k]
-            src = res[r][:, c].rearrange("b (q u e) -> b u q e", u=2, e=2)
-            if eng == "s":
-                nc.scalar.copy(out=dst, in_=src)
-            elif eng == "g":
-                nc.gpsimd.tensor_scalar(out=dst, in0=src, scalar1=1.0, scalar2=0.0, op0=ALU.mult, op1=ALU.add)
-            else:
-                nc.vector.tensor_copy(out=dst, in_=src)
+        def round_once(r, copy, c=None):
+            tile = row_tile(rounded, r, "rounded", BF16)
+            columns = slice(0, N) if c is None else half(c)
+            quads = slice(0, N // PACK) if c is None else chunk(c)
+            copy(
+                out=tile[:].rearrange("b (u q e) -> b u q e", u=2, e=2)[:, :, quads],
+                in_=result[r][:, columns].rearrange("b (q u e) -> b u q e", u=2, e=2),
+            )
 
-        def r_transpose(r, nh=None):
-            if r not in rt:
-                rt[r] = ps_2.tile([P, 2, 2, P], F32, name="rt", tag="turn")
-            words = rb[r][:].bitcast(F32)
-            for gg in range(2) if nh is None else (nh,):
-                for uu in range(2):
-                    k = 256 * uu + P * gg
-                    nc.tensor.transpose(rt[r][:, gg, uu, :], words[:, k : k + P], ident[:])
+        def plane_transpose(r, halves=range(HALVES)):
+            if r not in turned:
+                turned[r] = banks.tile([P, HALVES, 2, P], F32, name="turned")
+            words = rounded[r][:].bitcast(F32)
+            for c in halves:
+                for u in range(2):
+                    nc.tensor.transpose(turned[r][:, c, u, :], words[:, chunk(2 * u + c)], ident[:])
 
-        def r_copy(r, eng="s", nh=None):
+        def plane_interleave(r, copy, halves=slice(0, HALVES)):
             pair, k = r // 2, r % 2
-            if pair not in pg:
-                pg[pair] = st.tile([P, 2, 2 * P, 4], BF16, name="pg", align_bytes=64)
-            words = pg[pair][:].rearrange("p g b t -> p (g b t)").bitcast(F32).rearrange("p (g b u) -> p g b u", g=2, u=2)
-            h = slice(0, 2) if nh is None else slice(nh, nh + 1)
-            dst = words[:, h, P * k : P * (k + 1), :]
-            src = rt[r][:, h].rearrange("p g u b -> p g b u")
-            if eng == "s":
-                nc.scalar.copy(out=dst, in_=src)
-            else:
-                nc.vector.tensor_copy(out=dst, in_=src)
-
-        def r_quant(pair, k=None, nh=None):
-            if pair not in pq:
-                pq[pair] = st.tile([P, 2, 2 * P], U32, name="pq", align_bytes=64)
-                psc[pair] = st.tile([P, 2, 2 * P], U8, name="psc", align_bytes=64)
-            if k is None:
-                nc.vector.quantize_mx(
-                    out=pq[pair][:].rearrange("p g m -> p (g m)").bitcast(FP8X4),
-                    scales=psc[pair][:].rearrange("p g m -> p (g m)"),
-                    in_=pg[pair][:].rearrange("p g b t -> p (g b t)"),
-                )
-                return
-            m = slice(P * k, P * (k + 1))
-            nc.vector.quantize_mx(
-                out=pq[pair][:, nh, m].bitcast(FP8X4),
-                scales=psc[pair][:, nh, m],
-                in_=pg[pair][:, nh, m, :].rearrange("p b t -> p (b t)"),
+            if pair not in plane_words:
+                plane_words[pair] = two.tile([P, HALVES, 2 * P, PACK], BF16, name="plane_words", align_bytes=64)
+            copy(
+                out=by_word(plane_words[pair])[:, halves, chunk(k), :],
+                in_=turned[r][:, halves].rearrange("p g u b -> p g b u"),
             )
 
-        def store_words(pair, k=None):
-            lo, hi = (0, 2 * P) if k is None else (P * k, P * (k + 1))
+        def plane_tiles(pair):
+            if pair not in plane_codes:
+                plane_codes[pair] = two.tile([P, HALVES, 2 * P], U32, name="plane_codes", align_bytes=64)
+                plane_scales[pair] = two.tile([P, HALVES, 2 * P], U8, name="plane_scales", align_bytes=64)
+            return plane_codes[pair], plane_scales[pair]
+
+        def plane_quantise(pair):
+            codes, scales = plane_tiles(pair)
+            nc.vector.quantize_mx(
+                out=codes[:].rearrange("p g m -> p (g m)").bitcast(FP8X4),
+                scales=scales[:].rearrange("p g m -> p (g m)"),
+                in_=plane_words[pair][:].rearrange("p g b t -> p (g b t)"),
+            )
+
+        def plane_quantise_part(pair, k, c):
+            codes, scales = plane_tiles(pair)
+            nc.vector.quantize_mx(
+                out=codes[:, c, chunk(k)].bitcast(FP8X4),
+                scales=scales[:, c, chunk(k)],
+                in_=plane_words[pair][:, c, chunk(k), :].rearrange("p b t -> p (b t)"),
+            )
+
+        def store_codes(pair, columns=slice(0, 2 * P)):
+            words = out_1.rearrange("g p m t -> p g (m t)").bitcast(I32)
             nc.sync.dma_start(
-                out=out_1.rearrange("g p m t -> p g (m t)").bitcast(I32)[:, :, 2 * P * pair + lo : 2 * P * pair + hi],
-                in_=pq[pair][:, :, lo:hi].bitcast(I32),
+                out=words[:, :, 2 * P * pair + columns.start : 2 * P * pair + columns.stop],
+                in_=plane_codes[pair][:, :, columns].bitcast(I32),
             )
 
         def store_scales(pair):
+            width = 2 * P // 4
             for q in range(4):
+                live = plane_scales[pair][32 * q : 32 * q + 4].rearrange("p g m -> p (g m)").bitcast(I32)
                 nc.sync.dma_start(
-                    out=out_2.bitcast(I32)[:, 4 * q : 4 * q + 4, 64 * pair : 64 * (pair + 1)].rearrange("g r m -> r g m"),
-                    in_=psc[pair][32 * q : 32 * q + 4].rearrange("p g m -> p (g m)").bitcast(I32).rearrange("p (g m) -> p g m", g=2),
+                    out=out_2.bitcast(I32)[
+                        :, 4 * q : 4 * q + 4, width * pair : width * (pair + 1)
+                    ].rearrange("g r m -> r g m"),
+                    in_=live.rearrange("p (g m) -> p g m", g=HALVES),
                 )
 
-        def ok(r):
-            return 0 <= r < ROWS
-
         with tc.manual_schedule():
-            wh_interleave(*units[0], "v")
             x_transpose(0)
-            x_copy(0, "v")
-            x_transpose(1)
-            wh_quant(*units[0])
-            x_quant(0)
+            head_interleave(0, 0, on_vector)
+            x_interleave(0, on_scalar)
+            x_quantise(0)
             trunk(0)
-            x_copy(1, "s")
-            wh_interleave(*units[1], "v")
-            tanh(0)
-            wh_interleave(*units[2], "v")
-            x_quant(1)
-            wh_interleave(*units[3], "s")
+            tanh_trunk(0)
+            head_quantise(0, 0)
+            head_interleave(1, 1, on_vector)
             h_transpose(0)
+            x_transpose(1)
             h_gain(0)
-            wh_quant(*units[1])
-            h_quant(0)
-            wh_quant(*units[2])
+            x_interleave(1, on_vector)
+            head_interleave(1, 0, on_scalar)
+            head_quantise(1, 1)
+            x_quantise(1)
             trunk(1)
-            head(0, 0, 1)
-            tanh(1)
-            tanh1(0, 0)
+            head_interleave(0, 1, on_scalar)
+            h_quantise(0)
+            head_quantise(1, 0)
+            head_1(0, 0)
+            head_1(0, 1)
             x_transpose(2)
+            tanh_trunk(1)
+            head_interleave(2, 0, on_vector)
+            tanh_1(0, 0)
             h_transpose(1)
-            wh_interleave(*units[4], "v")
-            wh_quant(*units[3])
+            head_quantise(0, 1)
+            head_0(0, 0)
+            x_interleave(2, on_scalar)
+            head_quantise(2, 0)
             subtract(0, 0)
+            tanh_1(0, 1)
             x_transpose(3)
-            h_gain(1)
-            x_copy(2, "s")
+            head_0(0, 1)
+            exp_0(0, 0)
             square(0, 0)
-            head(0, 1, 1)
-            x_quant(2)
-            head(0, 1, 0)
-            tanh1(0, 1)
+            h_gain(1)
+            x_interleave(3, on_scalar)
+            exp_0(0, 1)
+            x_quantise(2)
+            head_2(0, 0)
             trunk(2)
-            head(0, 0, 0)
-            wh_interleave(*units[5], "v")
-            x_copy(3, "s")
-            h_quant(1)
-            exp0(0, 1)
-            wh_quant(*units[4])
-            exp0(0, 0)
-            subtract(0, 1)
-            tanh(2)
-            x_quant(3)
+            head_interleave(2, 1, on_vector)
+            h_quantise(1)
+            tanh_trunk(2)
+            head_quantise(2, 1)
             x_transpose(4)
-            wh_quant(*units[5])
-            head(1, 0, 0)
-            head(1, 1, 1)
-            head(0, 0, 2)
-            inv_half(0, 0)
-            x_transpose(5)
-            exp0(1, 0)
-            square(0, 1)
+            x_quantise(3)
+            head_1(1, 0)
+            inverse_p(0, 1)
+            inverse_p(0, 0)
+            subtract(0, 1)
+            tanh_1(1, 0)
             h_transpose(2)
-            head(1, 0, 1)
-            inv_half(0, 1)
-            weight_half(0, 0, "v")
-            x_copy(4, "s")
-            diff(0, 0)
-            tanh1(1, 0)
+            square(0, 1)
+            x_interleave(4, on_vector)
+            times_o(0, 0)
+            err_less_e(0, 0)
+            head_0(1, 0)
+            head_2(0, 1)
+            head_1(1, 1)
             h_gain(2)
-            head(0, 1, 2)
-            diff(0, 1)
-            weight_half(0, 1, "g")
-            tanh1(1, 1)
-            trunk(3)
-            head(1, 1, 0)
+            x_transpose(5)
+            err_less_e(0, 1)
+            exp_0(1, 0)
+            head_0(1, 1)
+            tanh_1(1, 1)
+            x_interleave(5, on_vector)
             subtract(1, 0)
-            tanh(3)
-            h_quant(2)
-            exp0(1, 1)
-            square(1, 0)
-            inv_half(1, 0)
-            x_quant(4)
-            prod(0)
-            x_copy(5, "s")
-            h_transpose(3)
-            head(2, 0, 0)
-            inv_half(1, 1)
-            weight_half(1, 0, "v")
+            trunk(3)
+            h_quantise(2)
+            x_quantise(4)
+            exp_0(1, 1)
+            head_1(2, 0)
+            head_0(2, 1)
+            inverse_p(1, 1)
             for s in range(1, 6):
-                exp0(s + 1, 0)
-                head(s + 1, 0, 1)
-                if ok(s - 2):
-                    store_r(s - 2, 0)
-                if ok(s - 2):
-                    store_r(s - 2, 1)
+                square(s, 0)
+                times_o(s - 1, 1)
+                weighted(s - 1)
                 subtract(s, 1)
-                result(s - 1, 0)
-                if ok(s + 5):
+                inverse_p(s, 0)
+                if s >= 4:
+                    plane_interleave(s - 4, on_scalar)
+                tanh_trunk(s + 2)
+                h_transpose(s + 2)
+                if s >= 5 and (s - 4) % 2 == 1:
+                    plane_quantise((s - 4) // 2)
+                add_e(s - 1, 1)
+                if s < ROWS - 5:
                     x_transpose(s + 5)
-                tanh1(s + 1, 0)
-                h_gain(s + 2)
-                result(s - 1, 1)
-                if ok(s + 4):
-                    x_quant(s + 4)
+                tanh_1(s + 1, 0)
+                head_1(s + 1, 1)
+                add_e(s - 1, 0)
+                exp_0(s + 1, 1)
                 square(s, 1)
-                head(s + 1, 1, 0)
-                head(s, 0, 2)
-                head(s + 1, 1, 1)
-                head(s, 1, 2)
-                weight_half(s, 1, "g")
-                diff(s, 0)
-                if ok(s - 2):
-                    round_r(s - 2, "s")
-                if ok(s - 4):
-                    r_copy(s - 4, "s")
-                h_quant(s + 2)
-                diff(s, 1)
-                if ok(s + 3):
-                    trunk(s + 3)
-                if ok(s + 5):
-                    x_copy(s + 5, "s")
+                head_0(s + 1, 0)
+                head_2(s, 1)
+                h_gain(s + 2)
+                if s >= 3:
+                    round_once(s - 3, on_scalar)
+                if s < ROWS - 5:
+                    x_interleave(s + 5, on_scalar)
+                head_2(s, 0)
                 subtract(s + 1, 0)
-                tanh1(s + 1, 1)
-                inv_half(s + 1, 0)
-                prod(s)
-                exp0(s + 1, 1)
-                if ok(s - 2):
-                    r_transpose(s - 2)
-                head(s + 2, 0, 0)
-                if ok(s + 3):
-                    tanh(s + 3)
-                weight_half(s + 1, 0, "v")
-                if (s - 4) % 2 == 1 and s - 4 > 0:
-                    r_quant((s - 4) // 2)
-                inv_half(s + 1, 1)
-                square(s + 1, 0)
-                if (s - 4) % 2 == 1 and s - 4 > 0:
+                if s >= 3:
+                    plane_transpose(s - 3)
+                exp_0(s + 1, 0)
+                err_less_e(s, 1)
+                err_less_e(s, 0)
+                h_quantise(s + 2)
+                times_o(s, 0)
+                tanh_1(s + 1, 1)
+                if s < ROWS - 3:
+                    trunk(s + 3)
+                if s >= 5 and (s - 4) % 2 == 1:
                     store_scales((s - 4) // 2)
-                if (s - 4) % 2 == 1 and s - 4 > 0:
-                    store_words((s - 4) // 2)
-                if ok(s + 3):
-                    h_transpose(s + 3)
+                head_1(s + 2, 0)
+                head_0(s + 2, 1)
+                if s < ROWS - 4:
+                    x_quantise(s + 4)
+                inverse_p(s + 1, 1)
+                if s >= 3:
+                    store_result(s - 3, 1)
+                if s >= 5 and (s - 4) % 2 == 1:
+                    store_codes((s - 4) // 2)
+                if s >= 2:
+                    store_result(s - 2, 0)
+            square(6, 0)
+            times_o(5, 1)
+            weighted(5)
+            store_result(4, 0)
+            add_e(5, 0)
+            store_result(4, 1)
+            round_once(3, on_scalar)
+            store_result(3, 1)
+            add_e(5, 1)
+            exp_0(7, 1)
             subtract(6, 1)
-            r_copy(3, "s")
-            store_r(4, 1)
-            exp0(7, 0)
-            result(5, 0)
+            head_2(6, 0)
             square(6, 1)
-            store_r(4, 0)
-            head(7, 0, 1)
-            head(7, 1, 0)
-            head(6, 0, 2)
-            result(5, 1)
-            head(6, 1, 2)
-            exp0(7, 1)
-            tanh1(7, 0)
-            diff(6, 0)
-            r_copy(2, "s")
-            inv_half(7, 0)
-            weight_half(6, 1, "g")
-            diff(6, 1)
-            weight_half(7, 0, "v")
-            prod(6)
+            inverse_p(6, 0)
+            head_2(6, 1)
+            plane_interleave(2, on_vector)
+            tanh_1(7, 0)
+            err_less_e(6, 0)
+            err_less_e(6, 1)
+            head_1(7, 1)
+            times_o(6, 1)
+            inverse_p(7, 1)
+            times_o(6, 0)
+            head_0(7, 0)
             subtract(7, 0)
-            r_quant(1)
-            head(7, 1, 1)
-            round_r(4, "s")
+            weighted(6)
+            round_once(5, on_scalar)
+            plane_transpose(3)
+            plane_interleave(3, on_vector)
+            tanh_1(7, 1)
             square(7, 0)
-            result(6, 0)
-            tanh1(7, 1)
-            r_transpose(4)
+            plane_transpose(5)
+            exp_0(7, 0)
+            times_o(7, 1)
             subtract(7, 1)
-            inv_half(7, 1)
-            result(6, 1)
-            r_copy(4, "s")
+            add_e(6, 0)
+            plane_quantise(1)
+            plane_interleave(5, on_scalar)
+            inverse_p(7, 0)
             square(7, 1)
-            round_r(5, "s")
-            store_r(5, 0)
-            store_r(6, 0)
-            round_r(6, "s")
-            head(7, 0, 2)
-            head(7, 1, 2)
-            diff(7, 0)
-            diff(7, 1)
-            r_transpose(5)
-            r_copy(5, "s")
-            weight_half(7, 1, "g")
-            r_transpose(6)
-            prod(7, 0)
-            prod(7, 1)
+            add_e(6, 1)
+            head_2(7, 0)
+            round_once(4, on_scalar)
+            head_2(7, 1)
+            round_once(6, on_scalar)
+            plane_transpose(4)
+            err_less_e(7, 0)
+            times_o(7, 0)
+            err_less_e(7, 1)
+            plane_interleave(4, on_scalar)
+            weighted(7, half(0))
+            plane_transpose(6)
+            plane_interleave(6, on_scalar)
+            store_result(6, 0)
+            weighted(7, half(1))
+            plane_quantise(2)
+            store_result(5, 0)
             store_scales(1)
-            store_r(6, 1)
-            r_copy(6, "s")
-            result(7, 0)
-            result(7, 1)
-            r_quant(2)
-            round_r(7, "s", 0)
-            round_r(7, "s", 1)
-            r_transpose(7, 0)
-            store_words(1)
-            r_transpose(7, 1)
-            r_copy(7, "v", 0)
-            store_r(5, 1)
-            r_quant(3, 0, 0)
-            r_quant(3, 0, 1)
-            r_copy(7, "s", 1)
-            r_quant(3, 1, 0)
-            store_r(7, 0)
-            store_r(7, 1)
-            store_words(2)
-            r_quant(3, 1, 1)
-            store_words(3, 0)
+            store_codes(1)
+            add_e(7, 0)
+            round_once(7, on_scalar, 0)
+            store_result(6, 1)
+            add_e(7, 1)
+            store_result(5, 1)
+            plane_transpose(7, (0,))
+            plane_quantise_part(3, 0, 0)
             store_scales(2)
-            store_words(3, 1)
+            store_codes(2)
+            round_once(7, on_vector, 1)
+            store_result(7, 0)
+            plane_transpose(7, (1,))
+            store_result(7, 1)
+            plane_interleave(7, on_scalar, slice(1, 2))
+            plane_interleave(7, on_vector, slice(0, 1))
+            plane_quantise_part(3, 0, 1)
+            plane_quantise_part(3, 1, 0)
+            store_codes(3, chunk(0))
+            plane_quantise_part(3, 1, 1)
+            store_codes(3, chunk(1))
             store_scales(3)

from contextlib import ExitStack

import concourse.mybir as mybir
from concourse.masks import make_identity

F32 = mybir.dt.float32
BF16 = mybir.dt.bfloat16
U32 = mybir.dt.uint32
I32 = mybir.dt.int32
U8 = mybir.dt.uint8
FP8X4 = mybir.dt.float8_e4m3fn_x4
FP4X4 = mybir.dt.float4_e2m1fn_x4
ACT = mybir.ActivationFunctionType
ALU = mybir.AluOpType

P = 128
PACK = 4
B, D, H, N, HEADS = 1024, 1024, 512, 1024, 3
GROUP = P * PACK
X_GROUPS = D // GROUP
HALF = 512
HALVES = N // HALF
ROWS = B // P
P_FLOOR = 0.2
FLOPS = 2 * B * D * H + HEADS * 2 * B * H * N


def tile_escmdoublyrobusterrormap_x2_kernel(tc, x, w_words, w_scales, g, wh, o, y, out_0, out_1, out_2):
    nc = tc.nc
    on_vector, on_scalar = nc.vector.tensor_copy, nc.scalar.copy

    with ExitStack() as ctx:
        const = ctx.enter_context(tc.tile_pool(name="const", bufs=1))
        blocks = ctx.enter_context(tc.tile_pool(name="blocks", bufs=ROWS))
        raw_heads = ctx.enter_context(tc.tile_pool(name="raw_heads", bufs=2))
        head_pairs = ctx.enter_context(tc.tile_pool(name="head_pairs", bufs=HEADS * HALVES))
        two = ctx.enter_context(tc.tile_pool(name="two", bufs=2))
        three = ctx.enter_context(tc.tile_pool(name="three", bufs=3))
        bank = ctx.enter_context(tc.psum_pool(name="bank", bufs=1))
        banks = ctx.enter_context(tc.psum_pool(name="banks", bufs=2))

        ident = const.tile([P, P], F32, name="ident", align_bytes=64)
        minus_two = const.tile([P, P], BF16, name="minus_two", align_bytes=64)
        first = const.tile([P, 1], F32, name="first")
        w_codes = const.tile([P, X_GROUPS, 2 * H], U8, name="w_codes", align_bytes=64)
        w_plane = const.tile([P, X_GROUPS, H], U8, name="w_plane", align_bytes=64)
        gain = const.tile([P, PACK], BF16, name="gain", align_bytes=64)

        nc.vector.memset(w_plane[:].rearrange("p g n -> p (g n)").bitcast(I32), 0)
        nc.vector.memset(first[:], 0.0)
        make_identity(nc, ident[:])
        nc.scalar.activation(out=first[:], in_=first[:], func=ACT.Exp)
        nc.vector.tensor_scalar(out=minus_two[:], in0=ident[:], scalar1=-2.0, scalar2=None, op0=ALU.mult)

        def half(c):
            return slice(HALF * c, HALF * (c + 1))

        def chunk(i):
            return slice(P * i, P * (i + 1))

        x_sb, o_sb, y_sb, wh_raw = {}, {}, {}, {}

        def load_x(r):
            x_sb[r] = blocks.tile([P, D], BF16, name="x_sb", align_bytes=64)
            nc.sync.dma_start(out=x_sb[r][:], in_=x[chunk(r), :])

        def load_oy(r):
            o_sb[r] = blocks.tile([P, N], BF16, name="o_sb", align_bytes=64)
            nc.sync.dma_start(out=o_sb[r][:], in_=o[chunk(r), :])
            y_sb[r] = blocks.tile([P, N], BF16, name="y_sb", align_bytes=64)
            nc.sync.dma_start(out=y_sb[r][:], in_=y[chunk(r), :])

        def load_head_half(t, c):
            raw = raw_heads.tile([P, PACK, HALF], BF16, name="raw_half", align_bytes=64)
            nc.sync.dma_start(out=raw[:], in_=wh[t].rearrange("(p j) n -> p j n", j=PACK)[:, :, half(c)])
            wh_raw[t, c] = raw[:]

        def load_head(t):
            raw = raw_heads.tile([P, PACK, N], BF16, name="raw_head", align_bytes=64)
            nc.sync.dma_start(out=raw[:], in_=wh[t].rearrange("(p j) n -> p j n", j=PACK))
            for c in range(HALVES):
                wh_raw[t, c] = raw[:, :, half(c)]

        def load_w_scales():
            for q in range(4):
                rows = w_plane[32 * q : 32 * q + 4].rearrange("p g n -> p (g n)").bitcast(I32)
                nc.sync.dma_start(
                    out=rows.rearrange("p (g n) -> p g n", g=X_GROUPS),
                    in_=w_scales.bitcast(I32)[:, 4 * q : 4 * q + 4, :].rearrange("g r n -> r g n"),
                )

        def load_w_codes():
            words = w_codes[:].rearrange("p g n -> p (g n)").bitcast(I32)
            nc.sync.dma_start(
                out=words.rearrange("p (g n) -> p g n", g=X_GROUPS),
                in_=w_words.bitcast(I32).rearrange("g p n -> p g n"),
            )

        def load_gain():
            nc.sync.dma_start(out=gain[:], in_=g.rearrange("(p t) -> p t", t=PACK))

        load_head_half(0, 0)
        load_x(0)
        load_w_scales()
        load_w_codes()
        load_head(1)
        load_x(1)
        load_gain()
        load_head_half(0, 1)
        load_head(2)
        load_x(2)
        load_oy(0)
        load_x(3)
        for r in range(1, ROWS):
            load_oy(r)
            if r + 3 < ROWS:
                load_x(r + 3)

        wh_words, wh_codes, wh_scales = {}, {}, {}

        def head_interleave(t, c, copy):
            wh_words[t, c] = head_pairs.tile([P, HALF, PACK], BF16, name="wh_words", align_bytes=64)
            copy(
                out=wh_words[t, c][:].rearrange("p (n i) j -> p n j i", i=4),
                in_=wh_raw[t, c].rearrange("p j (n i) -> p n j i", i=4),
            )

        def head_quantise(t, c):
            wh_codes[t, c] = const.tile([P, HALF], U32, name="wh_codes_%d_%d" % (t, c), align_bytes=64)
            wh_scales[t, c] = const.tile([P, HALF], U8, name="wh_scales_%d_%d" % (t, c), align_bytes=64)
            nc.vector.quantize_mx(
                out=wh_codes[t, c][:].bitcast(FP8X4),
                scales=wh_scales[t, c][:],
                in_=wh_words[t, c][:].rearrange("p n j -> p (n j)"),
            )

        x_turned, x_words, x_codes, x_scales = {}, {}, {}, {}
        trunk_sum, trunk_tanh, trunk_turned, h_words, h_codes, h_scales = {}, {}, {}, {}, {}, {}

        def by_word(tile):
            words = tile[:].rearrange("p g b t -> p (g b t)").bitcast(F32)
            return words.rearrange("p (g b u) -> p g b u", g=2, u=2)

        def x_transpose(r):
            x_turned[r] = banks.tile([P, X_GROUPS, 2, P], F32, name="x_turned", tag="turned")
            words = x_sb[r][:].bitcast(F32)
            for gg in range(X_GROUPS):
                for u in range(2):
                    pairs = words[:, 256 * gg + u : 256 * (gg + 1) : 2]
                    nc.tensor.transpose(x_turned[r][:, gg, u, :], pairs, ident[:])

        def x_interleave(r, copy):
            x_words[r] = two.tile([P, X_GROUPS, P, PACK], BF16, name="x_words", align_bytes=64)
            copy(out=by_word(x_words[r]), in_=x_turned[r][:].rearrange("p g u b -> p g b u"))

        def x_quantise(r):
            x_codes[r] = two.tile([P, X_GROUPS * P], U32, name="x_codes", align_bytes=64)
            x_scales[r] = two.tile([P, X_GROUPS * P], U8, name="x_scales", align_bytes=64)
            nc.vector.quantize_mx(
                out=x_codes[r][:].bitcast(FP8X4),
                scales=x_scales[r][:],
                in_=x_words[r][:].rearrange("p g b t -> p (g b t)"),
            )

        def trunk(r):
            trunk_sum[r] = bank.tile([P, H], F32, name="trunk_sum", tag="trunk")
            for gg in range(X_GROUPS):
                nc.tensor.matmul_mx(
                    out=trunk_sum[r][:],
                    lhsT=x_codes[r][:, chunk(gg)].bitcast(FP8X4),
                    lhsT_scale=x_scales[r][:, chunk(gg)],
                    rhs=w_codes[:, gg, :].bitcast(FP4X4),
                    rhs_scale=w_plane[:, gg, :],
                    start=(gg == 0),
                    stop=(gg == X_GROUPS - 1),
                )

        def tanh_trunk(r):
            trunk_tanh[r] = two.tile([P, PACK, P], F32, name="trunk_tanh", align_bytes=64)
            nc.scalar.activation(
                out=trunk_tanh[r][:], in_=trunk_sum[r][:].rearrange("b (p t) -> b t p", t=PACK), func=ACT.Tanh
            )

        def h_transpose(r):
            trunk_turned[r] = bank.tile([P, PACK, P], F32, name="trunk_turned", tag="trunk")
            for t in range(PACK):
                nc.tensor.transpose(trunk_turned[r][:, t, :], trunk_tanh[r][:, t, :], ident[:])

        def h_gain(r):
            h_words[r] = two.tile([P, P, PACK], BF16, name="h_words", align_bytes=64)
            nc.vector.tensor_tensor(
                out=h_words[r][:],
                in0=trunk_turned[r][:].rearrange("p t b -> p b t"),
                in1=gain[:].unsqueeze(1).to_broadcast([P, P, PACK]),
                op=ALU.mult,
            )

        def h_quantise(r):
            h_codes[r] = three.tile([P, P], U32, name="h_codes", align_bytes=64)
            h_scales[r] = three.tile([P, P], U8, name="h_scales", align_bytes=64)
            nc.vector.quantize_mx(
                out=h_codes[r][:].bitcast(FP8X4),
                scales=h_scales[r][:],
                in_=h_words[r][:].rearrange("p b t -> p (b t)"),
            )

        z, difference = {}, {}
        weight, z1_tanh, err, delta, result = {}, {}, {}, {}, {}

        def row_tile(store, r, name, dtype=F32):
            if r not in store:
                store[r] = three.tile([P, N], dtype, name=name, align_bytes=64)
            return store[r]

        def head_0(r, c):
            head_product(r, c, 0, "z01")

        def head_2(r, c):
            head_product(r, c, 2, "z2")

        def head_product(r, c, t, tag):
            z[r, c, t] = banks.tile([P, HALF], F32, name="z_%d" % t, tag=tag)
            nc.tensor.matmul_mx(
                out=z[r, c, t][:],
                lhsT=h_codes[r][:].bitcast(FP8X4),
                lhsT_scale=h_scales[r][:],
                rhs=wh_codes[t, c][:].bitcast(FP8X4),
                rhs_scale=wh_scales[t, c][:],
                start=True,
                stop=True,
            )

        def head_1(r, c):
            z[r, c, 1] = banks.tile([P, HALF], F32, name="z_1", tag="z01")
            for i in range(HALF // P):
                nc.tensor.matmul_mx(
                    out=z[r, c, 1][:, chunk(i)],
                    lhsT=wh_codes[1, c][:, chunk(i)].bitcast(FP8X4),
                    lhsT_scale=wh_scales[1, c][:, chunk(i)],
                    rhs=h_codes[r][:].bitcast(FP8X4),
                    rhs_scale=h_scales[r][:],
                    start=True,
                    stop=True,
                )

        def exp_0(r, c):
            tile = row_tile(weight, r, "weight")
            nc.scalar.activation(out=tile[:, half(c)], in_=z[r, c, 0][:], func=ACT.Exp, scale=-1.0)

        def tanh_1(r, c):
            tile = row_tile(z1_tanh, r, "z1_tanh")
            nc.scalar.activation(out=tile[:, half(c)], in_=z[r, c, 1][:], func=ACT.Tanh, scale=0.5)

        def subtract(r, c):
            difference[r, c] = bank.tile([P, HALF], F32, name="difference")
            nc.tensor.matmul(
                difference[r, c][:], lhsT=minus_two[:], rhs=y_sb[r][:, half(c)], start=True, stop=False
            )
            last = HALF // P - 1
            for i in range(HALF // P):
                nc.tensor.matmul(
                    difference[r, c][:, chunk(i)],
                    lhsT=z1_tanh[r][:, chunk(HALF // P * c + i)],
                    rhs=ident[:],
                    is_transpose=True,
                    start=False,
                    stop=(i == last),
                )

        def square(r, c):
            tile = row_tile(err, r, "err")
            nc.scalar.activation(
                out=tile[:, half(c)], in_=difference[r, c][:], func=ACT.Square, scale=0.5, bias=0.5
            )

        def inverse_p(r, c):
            nc.vector.tensor_scalar(
                out=weight[r][:, half(c)],
                in0=weight[r][:, half(c)],
                scalar1=1.0,
                scalar2=1.0 / P_FLOOR,
                op0=ALU.add,
                op1=ALU.min,
            )

        def times_o(r, c):
            nc.gpsimd.tensor_tensor(
                out=weight[r][:, half(c)], in0=weight[r][:, half(c)], in1=o_sb[r][:, half(c)], op=ALU.mult
            )

        def err_less_e(r, c):
            tile = row_tile(delta, r, "delta")
            nc.vector.tensor_tensor(
                out=tile[:, half(c)], in0=err[r][:, half(c)], in1=z[r, c, 2][:], op=ALU.subtract
            )

        def weighted(r, columns=slice(0, N)):
            nc.vector.tensor_tensor(
                out=delta[r][:, columns], in0=weight[r][:, columns], in1=delta[r][:, columns], op=ALU.mult
            )

        def add_e(r, c):
            tile = row_tile(result, r, "result")
            nc.vector.tensor_tensor(
                out=tile[:, half(c)], in0=z[r, c, 2][:], in1=delta[r][:, half(c)], op=ALU.add
            )

        def store_result(r, c):
            nc.sync.dma_start(out=out_0[chunk(r), half(c)], in_=result[r][:, half(c)])

        rounded, turned, plane_words, plane_codes, plane_scales = {}, {}, {}, {}, {}

        def round_once(r, copy, c=None):
            tile = row_tile(rounded, r, "rounded", BF16)
            columns = slice(0, N) if c is None else half(c)
            quads = slice(0, N // PACK) if c is None else chunk(c)
            copy(
                out=tile[:].rearrange("b (u q e) -> b u q e", u=2, e=2)[:, :, quads],
                in_=result[r][:, columns].rearrange("b (q u e) -> b u q e", u=2, e=2),
            )

        def plane_transpose(r, halves=range(HALVES)):
            if r not in turned:
                turned[r] = banks.tile([P, HALVES, 2, P], F32, name="turned")
            words = rounded[r][:].bitcast(F32)
            for c in halves:
                for u in range(2):
                    nc.tensor.transpose(turned[r][:, c, u, :], words[:, chunk(2 * u + c)], ident[:])

        def plane_interleave(r, copy, halves=slice(0, HALVES)):
            pair, k = r // 2, r % 2
            if pair not in plane_words:
                plane_words[pair] = two.tile([P, HALVES, 2 * P, PACK], BF16, name="plane_words", align_bytes=64)
            copy(
                out=by_word(plane_words[pair])[:, halves, chunk(k), :],
                in_=turned[r][:, halves].rearrange("p g u b -> p g b u"),
            )

        def plane_tiles(pair):
            if pair not in plane_codes:
                plane_codes[pair] = two.tile([P, HALVES, 2 * P], U32, name="plane_codes", align_bytes=64)
                plane_scales[pair] = two.tile([P, HALVES, 2 * P], U8, name="plane_scales", align_bytes=64)
            return plane_codes[pair], plane_scales[pair]

        def plane_quantise(pair):
            codes, scales = plane_tiles(pair)
            nc.vector.quantize_mx(
                out=codes[:].rearrange("p g m -> p (g m)").bitcast(FP8X4),
                scales=scales[:].rearrange("p g m -> p (g m)"),
                in_=plane_words[pair][:].rearrange("p g b t -> p (g b t)"),
            )

        def plane_quantise_part(pair, k, c):
            codes, scales = plane_tiles(pair)
            nc.vector.quantize_mx(
                out=codes[:, c, chunk(k)].bitcast(FP8X4),
                scales=scales[:, c, chunk(k)],
                in_=plane_words[pair][:, c, chunk(k), :].rearrange("p b t -> p (b t)"),
            )

        def store_codes(pair, columns=slice(0, 2 * P)):
            words = out_1.rearrange("g p m t -> p g (m t)").bitcast(I32)
            nc.sync.dma_start(
                out=words[:, :, 2 * P * pair + columns.start : 2 * P * pair + columns.stop],
                in_=plane_codes[pair][:, :, columns].bitcast(I32),
            )

        def store_scales(pair):
            width = 2 * P // 4
            for q in range(4):
                live = plane_scales[pair][32 * q : 32 * q + 4].rearrange("p g m -> p (g m)").bitcast(I32)
                nc.sync.dma_start(
                    out=out_2.bitcast(I32)[
                        :, 4 * q : 4 * q + 4, width * pair : width * (pair + 1)
                    ].rearrange("g r m -> r g m"),
                    in_=live.rearrange("p (g m) -> p g m", g=HALVES),
                )

        with tc.manual_schedule():
            x_transpose(0)
            head_interleave(0, 0, on_vector)
            x_interleave(0, on_scalar)
            x_quantise(0)
            trunk(0)
            tanh_trunk(0)
            head_quantise(0, 0)
            head_interleave(1, 1, on_vector)
            h_transpose(0)
            x_transpose(1)
            h_gain(0)
            x_interleave(1, on_vector)
            head_interleave(1, 0, on_scalar)
            head_quantise(1, 1)
            x_quantise(1)
            trunk(1)
            head_interleave(0, 1, on_scalar)
            h_quantise(0)
            head_quantise(1, 0)
            head_1(0, 0)
            head_1(0, 1)
            x_transpose(2)
            tanh_trunk(1)
            head_interleave(2, 0, on_vector)
            tanh_1(0, 0)
            h_transpose(1)
            head_quantise(0, 1)
            head_0(0, 0)
            x_interleave(2, on_scalar)
            head_quantise(2, 0)
            subtract(0, 0)
            tanh_1(0, 1)
            x_transpose(3)
            head_0(0, 1)
            exp_0(0, 0)
            square(0, 0)
            h_gain(1)
            x_interleave(3, on_scalar)
            exp_0(0, 1)
            x_quantise(2)
            head_2(0, 0)
            trunk(2)
            head_interleave(2, 1, on_vector)
            h_quantise(1)
            tanh_trunk(2)
            head_quantise(2, 1)
            x_transpose(4)
            x_quantise(3)
            head_1(1, 0)
            inverse_p(0, 1)
            inverse_p(0, 0)
            subtract(0, 1)
            tanh_1(1, 0)
            h_transpose(2)
            square(0, 1)
            x_interleave(4, on_vector)
            times_o(0, 0)
            err_less_e(0, 0)
            head_0(1, 0)
            head_2(0, 1)
            head_1(1, 1)
            h_gain(2)
            x_transpose(5)
            err_less_e(0, 1)
            exp_0(1, 0)
            head_0(1, 1)
            tanh_1(1, 1)
            x_interleave(5, on_vector)
            subtract(1, 0)
            trunk(3)
            h_quantise(2)
            x_quantise(4)
            exp_0(1, 1)
            head_1(2, 0)
            head_0(2, 1)
            inverse_p(1, 1)
            for s in range(1, 6):
                square(s, 0)
                times_o(s - 1, 1)
                weighted(s - 1)
                subtract(s, 1)
                inverse_p(s, 0)
                if s >= 4:
                    plane_interleave(s - 4, on_scalar)
                tanh_trunk(s + 2)
                h_transpose(s + 2)
                if s >= 5 and (s - 4) % 2 == 1:
                    plane_quantise((s - 4) // 2)
                add_e(s - 1, 1)
                if s < ROWS - 5:
                    x_transpose(s + 5)
                tanh_1(s + 1, 0)
                head_1(s + 1, 1)
                add_e(s - 1, 0)
                exp_0(s + 1, 1)
                square(s, 1)
                head_0(s + 1, 0)
                head_2(s, 1)
                h_gain(s + 2)
                if s >= 3:
                    round_once(s - 3, on_scalar)
                if s < ROWS - 5:
                    x_interleave(s + 5, on_scalar)
                head_2(s, 0)
                subtract(s + 1, 0)
                if s >= 3:
                    plane_transpose(s - 3)
                exp_0(s + 1, 0)
                err_less_e(s, 1)
                err_less_e(s, 0)
                h_quantise(s + 2)
                times_o(s, 0)
                tanh_1(s + 1, 1)
                if s < ROWS - 3:
                    trunk(s + 3)
                if s >= 5 and (s - 4) % 2 == 1:
                    store_scales((s - 4) // 2)
                head_1(s + 2, 0)
                head_0(s + 2, 1)
                if s < ROWS - 4:
                    x_quantise(s + 4)
                inverse_p(s + 1, 1)
                if s >= 3:
                    store_result(s - 3, 1)
                if s >= 5 and (s - 4) % 2 == 1:
                    store_codes((s - 4) // 2)
                if s >= 2:
                    store_result(s - 2, 0)
            square(6, 0)
            times_o(5, 1)
            weighted(5)
            store_result(4, 0)
            add_e(5, 0)
            store_result(4, 1)
            round_once(3, on_scalar)
            store_result(3, 1)
            add_e(5, 1)
            exp_0(7, 1)
            subtract(6, 1)
            head_2(6, 0)
            square(6, 1)
            inverse_p(6, 0)
            head_2(6, 1)
            plane_interleave(2, on_vector)
            tanh_1(7, 0)
            err_less_e(6, 0)
            err_less_e(6, 1)
            head_1(7, 1)
            times_o(6, 1)
            inverse_p(7, 1)
            times_o(6, 0)
            head_0(7, 0)
            subtract(7, 0)
            weighted(6)
            round_once(5, on_scalar)
            plane_transpose(3)
            plane_interleave(3, on_vector)
            tanh_1(7, 1)
            square(7, 0)
            plane_transpose(5)
            exp_0(7, 0)
            times_o(7, 1)
            subtract(7, 1)
            add_e(6, 0)
            plane_quantise(1)
            plane_interleave(5, on_scalar)
            inverse_p(7, 0)
            square(7, 1)
            add_e(6, 1)
            head_2(7, 0)
            round_once(4, on_scalar)
            head_2(7, 1)
            round_once(6, on_scalar)
            plane_transpose(4)
            err_less_e(7, 0)
            times_o(7, 0)
            err_less_e(7, 1)
            plane_interleave(4, on_scalar)
            weighted(7, half(0))
            plane_transpose(6)
            plane_interleave(6, on_scalar)
            store_result(6, 0)
            weighted(7, half(1))
            plane_quantise(2)
            store_result(5, 0)
            store_scales(1)
            store_codes(1)
            add_e(7, 0)
            round_once(7, on_scalar, 0)
            store_result(6, 1)
            add_e(7, 1)
            store_result(5, 1)
            plane_transpose(7, (0,))
            plane_quantise_part(3, 0, 0)
            store_scales(2)
            store_codes(2)
            round_once(7, on_vector, 1)
            store_result(7, 0)
            plane_transpose(7, (1,))
            store_result(7, 1)
            plane_interleave(7, on_scalar, slice(1, 2))
            plane_interleave(7, on_vector, slice(0, 1))
            plane_quantise_part(3, 0, 1)
            plane_quantise_part(3, 1, 0)
            store_codes(3, chunk(0))
            plane_quantise_part(3, 1, 1)
            store_codes(3, chunk(1))
            store_scales(3)
